import numpy as np, ml_dtypes
CORES = [3,7,11,15,131,135,139,143]
N = 8
BF = ml_dtypes.bfloat16
def gentries(a):
    return np.ascontiguousarray(a.reshape(8, 16, -1).transpose(0, 2, 1)).reshape(8, -1)
def gtable(e):
    e = np.asarray(e); return np.ascontiguousarray(e.reshape(8, -1, 16).transpose(0, 2, 1)).reshape(128, -1).astype(np.int32)
E, LEN, NC, RO, DR, DG = 4096, 32, 128, 4, 3, 1
MOD = (4, 4, 4, 4)
KINDS = np.array([1, 1, 2, 15, 16]); WAYS = np.array([0, 1, 2]); ROWS16 = np.arange(16)
def some(rng, kd, rows):
    i = rng.choice(rows, kd.shape); j = (i + rng.integers(1, 16, kd.shape)) & 15; row = np.arange(16).reshape(1, 1, 16, 1)
    return np.where(kd == 1, row == i, np.where(kd == 2, (row == i) | (row == j), (kd == 16) | (row != i))), row == i
def soil(rng, s, x, rate, kinds, ways, rows):
    sh = x.shape[:2] + (1, x.shape[3]); hit = rng.random(sh) < rate; on, first = some(rng, rng.choice(kinds, sh), rows); on = on & hit
    way = rng.choice(ways, sh); dl = rng.integers(1, 4, sh) * (2 * rng.integers(0, 2, sh) - 1); dl = np.where(first, dl, -dl)
    y = x + dl; y = np.where(np.abs(y) > 7, x - dl, y)
    return np.where(on & (way != 1), -s, s), np.where(on & (way != 0), y, x)
def graph(rng):
    A = E // 16; a = np.arange(A); nx = np.zeros((A, 8), np.int64); w = 1
    for i in range(4):
        m = MOD[i]; z = (a // w) % m
        nx[:, 2 * i] = a + ((z + 1) % m - z) * w; nx[:, 2 * i + 1] = a + ((z - 1) % m - z) * w; w *= m
    tau = np.argsort(rng.random((A, 8)), axis=1); inv = np.argsort(tau, axis=1); hi = np.argsort(rng.random((8, E // 8)), axis=1)
    nm = 8 * hi[tau[:, :, None], 2 * a[:, None, None] + np.arange(2)] + tau[:, :, None]
    at = np.zeros(E, np.int64); dr = np.zeros(E, np.int64); at[nm] = a[:, None, None]; dr[nm] = np.arange(8)[None, :, None]
    far = nx[at, dr]; j = np.ascontiguousarray(inv[far].T)
    sq = np.concatenate([nm[at, j, rng.integers(0, 2, (8, E))], nm[nx[at, j], dr, rng.integers(0, 2, (8, E))]])
    h = rng.integers(0, 8, (N, 8, NC, LEN // 2)); d = np.concatenate([h, h ^ 1], axis=3); d = np.take_along_axis(d, np.argsort(rng.random(d.shape), axis=3), 3)
    c = np.zeros(d.shape, np.int64); p = rng.integers(0, A, (N, 8, NC)); t = rng.integers(0, 2, d.shape)
    for i in range(LEN):
        c[..., i] = nm[p, d[..., i], t[..., i]]; p = nx[p, d[..., i]]
    sg = 2 * rng.integers(0, 2, (N, 8, 16, A)) - 1; u = rng.integers(0, 8, (N, 8, 16, A))
    return sg[..., at] * sg[..., far], sg[..., at] * (u[..., at] - u[..., far]), sq, c
def pack(s, x, sq, c):
    return {"v": np.ascontiguousarray((16 * s + x).reshape(N, 128, E)).astype(np.float32).astype(BF), "sq": np.stack([sq] * N).astype(np.int32), "lp": np.stack([gtable(a.reshape(8, -1)) for a in c])}
def skew(rng, shape, w):
    z = (E * rng.random(shape) ** w).astype(np.int64)
    return np.where(rng.random(shape) < 0.5, z, E - 1 - z)
def signs(rng, *shape):
    return 2 * rng.integers(0, 2, shape) - 1
def setup_inputs(rng):
    s, x, sq, c = graph(rng)
    s, x = soil(rng, s, x, rng.choice(np.array([0.03, 0.08, 0.15, 0.22]), (N, 8, 1, 1)), KINDS, WAYS, ROWS16)
    return pack(s, x, sq, c)
def setup_inputs_near(rng):
    s, x, sq, c = graph(rng)
    for b, kinds, ways, rows in ((0, [1], [0], [15]), (1, [2], [1], list(range(16))), (2, [1], [1], [0, 7, 8, 15]), (3, [15, 16], [0, 1, 2], list(range(16)))):
        s[:, b::4], x[:, b::4] = soil(rng, s[:, b::4], x[:, b::4], 0.15, np.array(kinds), np.array(ways), np.array(rows))
    return pack(s, x, sq, c)
def setup_inputs_spread(rng):
    s = np.repeat(signs(rng, N, 8, 16, 1), 5, axis=3); x = np.repeat(rng.integers(-7, 8, (N, 8, 16, 1)), 5, axis=3)
    s[..., 1:3], x[..., 1:3] = soil(rng, s[..., 1:3], x[..., 1:3], 1.0, KINDS, WAYS, ROWS16)
    s[..., 3:] = signs(rng, N, 8, 16, 2); x[..., 3:] = rng.integers(-7, 8, (N, 8, 16, 2))
    who = (5 * rng.random((N, 8, E)) ** rng.choice(np.array([4.0, 8.0, 16.0]), (N, 8, 1))).astype(np.int64)[:, :, None, :]
    w = np.array([1.0, 2.0, 4.0])
    return pack(np.take_along_axis(s, who, 3), np.take_along_axis(x, who, 3), skew(rng, (16, E), rng.choice(w, (16, 1))), skew(rng, (N, 8, NC, LEN), rng.choice(w, (N, 8, 1, 1))))
def setup_inputs_ends(rng):
    M = E - 1; s0 = signs(rng, N, 8, 16, 1); x0 = 7 * s0 * np.where(rng.random(s0.shape) < 0.85, 1, -1)
    kd = rng.choice(np.array([1, 2, 15, 16]), (N, 8, 1, 2)); on, first = some(rng, kd, ROWS16); way = rng.integers(0, 3, kd.shape)
    s = np.concatenate([s0, np.where(on & (way != 2), -s0, s0)], axis=3); x = np.concatenate([x0, np.where(on & (way != 1), -x0, x0)], axis=3)
    who = rng.choice(np.array([0, 1, 2]), (N, 8, E), p=[0.7, 0.15, 0.15]); q = np.arange(N)[:, None]
    who[..., 0] = 0; who[..., M] = np.where((q + np.arange(8)) % 4 == 3, 1 + (q & 1), 0)
    s = np.take_along_axis(s, who[:, :, None, :], 3); x = np.take_along_axis(x, who[:, :, None, :], 3)
    s[:, 7, 15] = 1; x[:, 7, 15] = 7; s[:, 7, 0] = 1; x[:, 7, 0] = -7
    sq = np.where(rng.random((16, E)) < 0.72, M * rng.integers(0, 2, (16, E)), rng.integers(0, E, (16, E)))
    for e, k, f2, e2 in ((0, 0, 0, M), (0, 7, M, M), (M, 7, M, 0), (M, 0, 0, 0)):
        sq[k, e] = f2; sq[8 + k, e] = e2
    c = np.where(rng.random((N, 8, NC, LEN)) < 0.72, M * rng.integers(0, 2, (N, 8, NC, LEN)), rng.integers(0, E, (N, 8, NC, LEN)))
    return pack(s, x, sq, c)
def setup_inputs_corners(rng):
    M = E - 1; e = np.arange(E); reg = ((np.arange(N)[:, None] + np.arange(8) + rng.integers(0, 8)) % 8).reshape(N, 8, 1, 1)
    s = np.repeat(signs(rng, N, 8, 16, 1), E, axis=3); x = np.repeat(rng.integers(-7, 8, (N, 8, 16, 1)), E, axis=3)
    s, x = soil(rng, s, x, np.where(reg == 1, 0.15, 0.0), KINDS, WAYS, ROWS16)
    s, x = soil(rng, s, x, np.where(reg == 3, 0.25, 0.0), np.array([1, 16]), WAYS, ROWS16)
    s = np.where(reg == 2, signs(rng, N, 8, 16, E), s); x = np.where(reg == 2, rng.integers(-7, 8, (N, 8, 16, E)), x)
    row = np.arange(16).reshape(1, 1, 16, 1); own = rng.integers(0, 16, (N, 8, 1, 1)); low = np.minimum(own, 14); odd = (np.arange(N) & 1).reshape(N, 1, 1, 1) == 1
    two = rng.integers(0, 2, (N, 8, 1, E)); three = rng.integers(0, 3, (N, 8, 1, E))
    x = np.where((reg == 4) & (row == own), rng.integers(-3, 4, (N, 8, 1, 1)) + 4 - 8 * two, x)
    m = np.where(odd, rng.integers(1, 8, (N, 8, 1, 1)), 4)
    x = np.where((reg == 5) & (row == low), m * two, x); x = np.where((reg == 5) & (row == low + 1), -two, x); s = np.where((reg == 5) & ((row == low) | (row == low + 1)), 1, s)
    x = np.where((reg == 6) & (row == own), np.where(three > 0, 7, -7), x); s = np.where((reg == 6) & (row == own), np.where(three == 2, -1, 1), s)
    x = np.where((reg == 7) & (row == own), np.where(odd, 6 + two, -6 - two), x); s = np.where((reg == 7) & (row == own), 1, s)
    a = np.stack([e, 0 * e, 0 * e + M, (e + 1) % E, (e - 1) % E])
    sq = np.where(rng.random((16, E)) < 0.4, rng.integers(0, E, (16, E)), a[rng.integers(0, 5, (16, E)), e])
    b = rng.integers(0, E, (N, 8, NC, 1)); i = np.arange(LEN).reshape(1, 1, 1, LEN); z = np.zeros((N, 8, NC, LEN), np.int64)
    c = np.choose(rng.integers(0, 6, (N, 8, NC, 1)), [b + z, M * (i & 1) + z, (b + i) % E, rng.integers(0, E, z.shape), z, z + M])
    return pack(s, x, sq, c)
def setup_inputs_crowd(rng):
    s = np.repeat(signs(rng, N, 8, 16, 1), E, axis=3); x = np.repeat(rng.integers(-7, 8, (N, 8, 16, 1)), E, axis=3)
    s, x = soil(rng, s, x, 0.12, KINDS, WAYS, ROWS16)
    sq = rng.integers(0, E, (16, E)); c = rng.integers(0, E, (N, 8, NC, LEN)); o = int(rng.integers(0, 4))
    for q in range(N):
        for g in range(8):
            m = (q + g + o) % 4; n = rng.integers(0, E, 3)
            if m < 2: c[q, g] = n[0]
            if m == 1: c[q, g, (NC - 1, 0, int(rng.integers(0, NC)))[g % 3], (LEN - 1, 0)[q & 1]] = (int(n[0]) + 1 + int(rng.integers(0, E - 1))) % E
            if m == 2: c[q, g] = n[rng.integers(0, 3, (NC, LEN))]
    return pack(s, x, sq, c)
def check_inputs(d):
    bad = []; a = np.asarray(d["v"]).astype(np.float64)
    if not np.all((np.abs(a) >= 9) & (np.abs(a) <= 23) & (a == np.floor(a))): bad.append("range of v")
    for k in ("sq", "lp"):
        if np.min(d[k]) < 0 or np.max(d[k]) > E - 1: bad.append("range of " + k)
    if not np.all(np.asarray(d["sq"]) == np.asarray(d["sq"])[:1]): bad.append("sq alike on all ranks")
    return bad
def reference(v, sq, lp):
    w = v.astype(np.float32).astype(np.int64).reshape(N, 8, 16, E); tab = sq.astype(np.int64); q = np.arange(N).reshape(N, 1, 1, 1)
    c = np.stack([gentries(a) for a in lp]).astype(np.int64).reshape(N, 8, NC, LEN)
    def pick(names):
        a = np.take_along_axis(w, names.reshape(N, 8, 1, -1), 3); s = np.where(a > 0, 1, -1)
        return s, a - 16 * s
    for rnd in range(RO):
        par = rnd & 1; c = np.roll(c, -par, axis=3); e = c[..., 0::2]; f = c[..., 1::2]; k = f & 7
        f2 = tab[q, k, e]; e2 = tab[q, 8 + k, e]
        se, xe = pick(e); sf, xf = pick(f); sf2, xf2 = pick(f2); se2, xe2 = pick(e2)
        ok = np.all((xe + se * xf == xf2 + sf2 * xe2) & (se * sf == sf2 * se2), axis=2).reshape(e.shape)
        c = np.stack([np.where(ok, f2, e), np.where(ok, e2, f)], axis=4).reshape(N, 8, NC, LEN); c = np.roll(c, par, axis=3)
        c = np.roll(c, DR, axis=0); c[:, :, 1::2] = np.roll(c[:, :, 1::2], DG, axis=1)
    s, x = pick(c); s = s.reshape(N, 8, 16, NC, LEN); x = x.reshape(N, 8, 16, NC, LEN)
    before = np.concatenate([np.ones_like(s[..., :1]), np.multiply.accumulate(s, axis=4)[..., :-1]], axis=4)
    b = np.add.reduce(before * x, axis=4)
    return {"yc": np.stack([gtable(a.reshape(8, -1)) for a in c]).astype(np.float32), "yb": b.reshape(N, 128, NC).astype(np.float32)}

@@ -1,0 +1,408 @@
+from concourse.mybir import AluOpType, ActivationFunctionType
+
+RO = 4
+CH = [32, 32, 32, 32]
+NP = 4
+FIN = [1, 1, 1, 2]
+ACT_D = 0.4
+ORDER = [0, 1, 4, 5, 2, 3, 7, 9, 10, 11, 12, 13, 14, 52, 15, 49, 50, 6, 8, 17, 16, 55, 51, 18, 19, 21, 20, 41, 23, 36, 53, 22, 33, 76, 31, 54, 34, 25, 24, 27, 43, 26, 29, 44, 47, 32, 42, 56, 30, 28, 45, 37, 62, 38, 39, 35, 46, 99, 40, 84, 63, 79, 64, 122, 102, 80, 69, 75, 81, 70, 82, 103, 83, 86, 48, 85, 77, 72, 98, 65, 107, 87, 57, 66, 78, 104, 67, 100, 105, 68, 88, 73, 106, 121, 58, 89, 59, 60, 125, 90, 109, 61, 91, 126, 101, 92, 93, 110, 94, 145, 95, 127, 96, 123, 111, 128, 108, 97, 129, 112, 132, 148, 113, 124, 114, 144, 115, 116, 133, 117, 149, 118, 134, 146, 119, 168, 71, 120, 130, 150, 135, 151, 131, 152, 136, 171, 155, 137, 167, 138, 153, 139, 156, 140, 154, 147, 172, 141, 169, 142, 157, 143, 191, 173, 158, 174, 175, 159, 194, 178, 160, 190, 161, 176, 162, 179, 163, 170, 195, 164, 192, 165, 180, 74, 214, 166, 196, 181, 197, 177, 198, 182, 217, 201, 183, 213, 199, 184, 185, 202, 186, 218, 193, 200, 187, 215, 188, 203, 189, 237, 219, 204, 220, 221, 205, 240, 224, 206, 236, 245, 207, 222, 208, 225, 209, 216, 241, 210, 238, 211, 226, 260, 212, 242, 227, 243, 223, 244, 228, 263, 247, 246, 229, 259, 264, 230, 268, 231, 248, 232, 239, 233, 261, 234, 249, 235, 283, 265, 250, 266, 267, 251, 286, 270, 269, 252, 282, 287, 253, 254, 271, 255, 262, 256, 284, 257, 272, 306, 258, 288, 273, 289, 290, 274, 309, 293, 275, 305, 291, 276, 277, 294, 278, 310, 285, 292, 279, 307, 280, 295, 281, 329, 311, 296, 312, 313, 297, 314, 316, 332, 315, 328, 298, 333, 299, 300, 317, 301, 308, 302, 334, 318, 303, 330, 335, 352, 304, 336, 319, 339, 355, 320, 351, 321, 356, 340, 331, 322, 337, 357, 323, 358, 353, 341, 324, 338, 375, 325, 359, 326, 342, 362, 378, 327, 343, 374, 344, 379, 363, 354, 345, 380, 346, 381, 376, 364, 347, 348, 365, 349, 398, 382, 406, 350, 383, 360, 385, 401, 361, 366, 397, 367, 402, 386, 384, 377, 368, 403, 369, 404, 399, 370, 387, 421, 405, 388, 371, 408, 389, 424, 372, 373, 420, 409, 425, 407, 400, 426, 390, 427, 391, 428, 392, 410, 422, 393, 431, 411, 423, 394, 412, 432, 395, 396, 429, 433, 413, 430, 414, 415, 416, 445, 434, 417, 435, 418, 436, 437, 419, 447, 438, 446, 439, 458, 448, 440, 457, 441, 456, 442, 450, 449, 443, 451, 444, 459, 467, 468, 460, 461, 465, 454, 462, 469, 455, 466, 470, 488, 478, 476, 471, 477, 472, 479, 463, 452, 480, 464, 481, 487, 473, 453, 483, 482, 474, 490, 489, 475, 484, 491, 485, 492, 486, 493, 494, 495]
+
+SCRATCH = {
+    "vt": ("sbuf", [128, 4096], "bfloat16"),
+    "mt": ("sbuf", [128, 4096], "bfloat16"),
+    "sqt": ("sbuf", [128, 4096], "float32"),
+    "sqi": ("sbuf", [128, 512], "int32"),
+    "sqh": ("sbuf", [128, 512], "float16"),
+    "lpi": ("sbuf", [128, 520], "int32"),
+    "ones": ("sbuf", [128, 512], "bfloat16"),
+    "sel": ("sbuf", [128, 1024], "bfloat16"),
+    "zm": ("sbuf", [128, 2 * 144], "bfloat16"),
+    "pm": ("sbuf", [128, 11 * 160], "bfloat16"),
+    "mi": ("sbuf", [128, 64], "int32"),
+    "mj": ("sbuf", [128, 64], "int32"),
+    "sg": ("sbuf", [128, 4096], "bfloat16"),
+    "dd": ("sbuf", [128, 4096], "bfloat16"),
+    "hs": ("sbuf", [128, 4096], "bfloat16"),
+    "fx": ("sbuf", [128, 128], "bfloat16"),
+    "ycs": ("sbuf", [128, 256], "float32"),
+    "ybs": ("sbuf", [128, 128], "float32"),
+}
+for _r in range(RO + 1):
+    SCRATCH["lst%d" % _r] = ("sbuf", [128, 256], "uint16")
+for _r in range(RO):
+    for _n in ("s1", "a1", "a2", "a3", "b1", "b2", "ne"):
+        SCRATCH["%s_%d" % (_n, _r)] = ("sbuf", [128, 2048], "bfloat16")
+    SCRATCH["s2_%d" % _r] = ("sbuf", [128, 2048], "float16")
+    SCRATCH["prop%d" % _r] = ("sbuf", [128, 256], "uint16")
+    SCRATCH["snd%d" % _r] = ("sbuf", [128, 256], "uint16")
+    SCRATCH["old%d" % _r] = ("sbuf", [128, 256], "float16")
+    SCRATCH["xh%d" % _r] = ("sbuf", [128, 256], "float16")
+    SCRATCH["new%d" % _r] = ("sbuf", [128, 256], "float16")
+    SCRATCH["mm%d" % _r] = ("sbuf", [128, 256], "float32")
+    SCRATCH["ok%d" % _r] = ("sbuf", [128, 256], "float32")
+for _b in range(8):
+    SCRATCH["ps%d" % _b] = ("psum", [128, 512], "float32")
+
+SEMAPHORES = ["c_act", "c_dve", "c_pe", "c_pool", "in_sq", "in_lp", "in_v", "outs", "sent"] + \
+    ["arr%d_%d" % (r, c) for r in range(RO) for c in range(len(CH))]
+
+COST = {"g": 1.3, "f": 1.04, "fix": 55.0, "mm": 34.0, "hop": 80.0, "remote": 2600.0, "issue": 500.0, "dma": 2000.0,
+        "bw": 250.0}
+
+
+def build(T, g, dst_addr, out_mask, n_in, cost):
+    A = AluOpType
+    F = ActivationFunctionType
+    ops = []
+    last_w = {}
+    readers = {}
+    seq = [-1]
+    C0 = [sum(CH[:c]) for c in range(len(CH))]
+
+    def add(typ, eng, fn, reads, writes, dur, lat=0.0, sem=None, after=()):
+        deps = set(after)
+        for k in reads:
+            if k in last_w:
+                deps.add(last_w[k])
+        for k in writes:
+            if k in last_w:
+                deps.add(last_w[k])
+            deps.update(readers.get(k, ()))
+        i = len(ops)
+        deps.discard(i)
+        for k in reads:
+            readers.setdefault(k, []).append(i)
+        for k in writes:
+            last_w[k] = i
+            readers[k] = []
+        ops.append({"eng": eng, "fn": fn, "deps": sorted(deps), "dur": dur, "lat": lat, "sem": sem, "seq": seq[0],
+                    "typ": typ})
+        return i
+
+    def gath(n):
+        return cost["fix"] + cost["g"] * n
+
+    def plain(n, k=1.0):
+        return cost["fix"] * 0.3 + cost["f"] * max(64.0, k * n)
+
+    def pool(n):
+        return 170.0 + 2 * cost["f"] * n
+
+    def asel(typ, out, in_, pattern, op, base, cm, reads, writes, n):
+        add(typ, "pool", lambda: g.affine_select(out, in_, pattern, op, 0.0, base, cm), reads, writes, pool(n))
+
+    ps = [T["ps%d" % b] for b in range(8)]
+    add("ld0", "sync", lambda: g.sync.dma_start(T.sqi[:, :], T.sq[:, :]), [], ["sqi"], 100.0,
+        cost["dma"] + 262144 / cost["bw"], ("in_sq", 16))
+    add("ld1", "act", lambda: g.scalar.dma_start(T.lpi[0:128:2, 1:513], T.lp[:, :]), [], ["lpa"], 100.0,
+        cost["dma"] + 400000 / cost["bw"], ("in_lp", 32))
+    add("ld1", "act", lambda: g.scalar.dma_start(T.lpi[1:128:2, 0:512], T.lp[:, :]), [], ["lpb"], 100.0,
+        cost["dma"] + 520000 / cost["bw"], ("in_lp", 32))
+    add("ld2", "sync", lambda: g.sync.dma_start(T.vt[:, :], T.v[:, :]), [], ["vt"], 100.0,
+        cost["dma"] + 1570000 / cost["bw"], ("in_v", 16))
+    add("mi", "pool", lambda: g.iota(T.mi[:, :], [[-1, 64]], 128, 1), [], ["mi"], pool(64))
+    add("ones", "dve", lambda: g.vector.memset(T.ones[:, :], 1.0), [], ["ones"], plain(512, 0.5))
+    add("zm", "dve", lambda: g.vector.memset(T.zm[:, :], 0.0), [], ["zm0", "zm1"], plain(288, 0.5))
+    for hf in range(2):
+        asel("sel%d" % hf, T.sel[:, 512 * hf:512 * hf + 512], T.ones[:, :], [[-1, 4], [0, 8], [-8, 16]], A.is_equal,
+             -4 * hf, 1, ["ones"], ["sel%d" % hf], 512)
+    add("mt0", "dve", lambda: g.vector.tensor_scalar(T.mj[:, :], T.mi[:, :], 7, None, A.bitwise_and), ["mi"], ["mj"], plain(64))
+    add("mt0", "dve", lambda: g.vector.tensor_scalar(T.mt[:, 0:64], T.mj[:, :], 0.0, -1.0, A.is_equal, A.mult), ["mj"], ["mt0"],
+        plain(64))
+    n = 64
+    while n < 1024:
+        add("mt0", "dve", lambda n=n: g.vector.tensor_copy(T.mt[:, n:2 * n], T.mt[:, 0:n]), ["mt0"], ["mt0"], plain(n, 0.5))
+        n *= 2
+    add("mt1", "act", lambda: g.scalar.activation(T.mt[:, 1024:2048], T.mt[:, 0:1024], F.Copy), ["mt0"], ["mt1"], plain(1024))
+    add("mt2", "act", lambda: g.scalar.activation(T.mt[:, 2048:3072], T.mt[:, 0:1024], F.Copy), ["mt0"], ["mt2"], plain(1024))
+    add("mt3", "dve", lambda: g.vector.tensor_copy(T.mt[:, 3072:4096], T.mt[:, 0:1024]), ["mt0"], ["mt3"], plain(1024, 0.5))
+    MT = ["mt0", "mt1", "mt2", "mt3"]
+    add("sqh", "dve", lambda: g.vector.tensor_scalar(T.sqh[:, :], T.sqi[:, :], -2048.0, None, A.add), ["sqi"], ["sqh"],
+        plain(512))
+    for s in range(8):
+        add("sqm%d" % s, "pe", lambda s=s: g.tensor.matmul(ps[s][:, :], T.sel[:, 128 * s:128 * s + 128], T.sqh[:, :], True, True),
+            ["sel%d" % (s // 4), "sqh"], ["ps%d" % s], 8 * cost["mm"])
+        if s % 2 == 0:
+            add("sqe%d" % s, "act", lambda s=s: g.scalar.activation(T.sqt[:, 512 * s:512 * s + 512], ps[s][:, :], F.Copy),
+                [], ["ps%d" % s, "sqt%d" % s], plain(512))
+        else:
+            add("sqe%d" % s, "dve", lambda s=s: g.vector.tensor_copy(T.sqt[:, 512 * s:512 * s + 512], ps[s][:, :]),
+                [], ["ps%d" % s, "sqt%d" % s], plain(512))
+    SQT = ["sqt%d" % s for s in range(8)]
+    for c, nc in enumerate(CH):
+        for b in range(2):
+            s0 = 1 + 256 * b + 2 * C0[c]
+            d0 = 2 * C0[c] + nc * b
+            add("l0_%d" % c, "dve", lambda nc=nc, d0=d0, s0=s0: g.vector.tensor_copy(
+                T.lst0[:, d0:d0 + nc], T.lpi[:, s0:s0 + 2 * nc - 1:2]),
+                ["lpa", "lpb"], ["l0_%d_%d" % (c, b)], plain(nc))
+
+    for j, lo, hi in ((7, 0, 7), (15, 8, 15)):
+        col = T.zm[:, j:128:16]
+        asel("w0", col, T.ones[:, 0:8], [[-16, 8]], A.is_ge, -lo, 1, ["ones"], ["zm0"], 8)
+        asel("w0", col, col, [[16, 8]], A.is_ge, hi, -1, [], ["zm0"], 8)
+    col = T.zm[:, 144 + 7:144 + 128:8]
+    asel("w1", col, T.ones[:, 0:16], [[-16, 8], [0, 2]], A.is_ge, 0, 1, ["ones"], ["zm1"], 16)
+    asel("w1", col, col, [[16, 8], [0, 2]], A.is_ge, 15, -1, [], ["zm1"], 16)
+
+    def rowsum(k, a):
+        o = 144 * k + 7 - a
+        return T.zm[:, o:o + 128]
+
+    LO, HI, ID, FA, FB, LOP, HIP, FBP = 0, 1, 2, 3, 4, 5, 7, 9
+    base = {LO: 32, HI: 16, ID: 16, FA: 16, FB: 16, LOP: 32, LOP + 1: 32, HIP: 16, HIP + 1: 16, FBP: 16, FBP + 1: 16}
+
+    def mat(k, shift):
+        o = 160 * k + base[k] - shift
+        return T.pm[:, o:o + 128]
+
+    def diag(typ, k, d):
+        o, b = 160 * k, base[k]
+        kk = ["pm%d" % k]
+        asel(typ, T.pm[:, o:o + b], T.ones[:, 0:b], [[-1, b]], A.is_equal, b - 128 - d, 1, ["ones"], kk, b)
+        asel(typ, T.pm[:, o + b:o + 160], T.ones[:, 0:160 - b], [[-1, 160 - b]], A.is_equal, -d, 1, ["ones"], kk, 160 - b)
+
+    def keep(typ, k, src, pattern, op, bs):
+        asel(typ, T.pm[:, 160 * k:160 * k + 160], T.pm[:, 160 * src:160 * src + 160], pattern, op, bs, 0,
+             ["pm%d" % src], ["pm%d" % k], 160)
+
+    def column(typ, k, d, s):
+        o = 160 * k
+        kk = ["pm%d" % k]
+        asel(typ, T.pm[:, o + 16 + d:o + 144:16], T.ones[:, 0:8], [[-16, 8]], A.is_equal, -s, 1, ["ones"], kk, 8)
+        asel(typ, T.pm[:, o + d:o + d + 1], T.ones[:, 0:1], [[0, 1]], A.is_equal, -112 - s, 1, ["ones"], kk, 1)
+    diag("plo", LO, 0)
+    keep("plo", LO, LO, [[0, 10], [-1, 16]], A.is_ge, 7)
+    diag("pid", ID, 0)
+    keep("phi", HI, ID, [[0, 10], [1, 16]], A.is_ge, -8)
+    diag("pfa", FA, 2)
+    keep("pfa", FA, FA, [[0, 10], [-1, 16]], A.is_ge, 5)
+    column("pfa", FA, 14, 1)
+    column("pfa", FA, 15, 0)
+    diag("pfb", FB, -2)
+    keep("pfb", FB, FB, [[0, 10], [1, 16]], A.is_ge, -10)
+    column("pfb", FB, 1, 14)
+    column("pfb", FB, 0, 15)
+    for h in range(2):
+        for k, src in ((LOP, LO), (HIP, HI), (FBP, FB)):
+            keep("pz", k + h, src, [[0, 80], [1, 2]], A.is_equal, -h)
+
+    def round_chunk(r, c):
+        NC = CH[c]
+        W = 16 * NC
+        N2 = 2 * NC
+        L = T["lst%d" % r]
+        l0 = 2 * C0[c]
+        eL, fL, bL = L[:, l0:l0 + NC], L[:, l0 + NC:l0 + N2], L[:, l0:l0 + N2]
+        kE, kF = "l%d_%d_0" % (r, c), "l%d_%d_1" % (r, c)
+        w0 = 16 * C0[c]
+
+        def buf(nm, a=0, b=W):
+            return T["%s_%d" % (nm, r)][:, w0 + a:w0 + b]
+
+        def small(nm, a=0, b=N2, st=1):
+            return T["%s%d" % (nm, r)][:, l0 + a:l0 + b:st]
+
+        def key(nm):
+            return "%s_%d_%d" % (nm, r, c)
+        bp = seq[0] % NP
+        bb = NP + seq[0] % (8 - NP)
+        P = ps[bp]
+        kP = "ps%d" % bp
+        B = ps[bb][:, 0:W]
+        kB = "ps%d" % bb
+        s2 = T["s2_%d" % r]
+        ne = T["ne_%d" % r]
+        vt = T.vt[:, :]
+        add("a1", "act", lambda: g.scalar.activation(buf("a1"), vt.indirect(eL), F.Abs, bias=0.25), ["vt", kE], [key("a1")], gath(W))
+        add("s1", "act", lambda: g.scalar.activation(buf("s1"), T.mt[:, :].indirect(fL), F.Copy), MT + [kF],
+            [key("s1")], gath(W))
+        add("a2", "dve", lambda: g.vector.tensor_tensor(buf("a2"), vt.indirect(fL), buf("a1"), A.add),
+            ["vt", kF, key("a1")], [key("a2")], gath(W))
+        add("a3", "act", lambda: g.scalar.activation(buf("a3"), buf("a2"), F.Abs, bias=-16.0), [key("a2")], [key("a3")],
+            plain(W))
+        add("s2", "dve", lambda: g.vector.tensor_tensor(buf("s2"), T.sqt[:, :].indirect(eL), buf("s1"), A.mult),
+            SQT + [kE, key("s1")], [key("s2")], gath(W))
+
+        def f_x():
+            ins = None
+            for a in range(8):
+                ins = g.tensor.matmul(P[:, 0:N2], rowsum(0, a), s2[:, w0 + a:w0 + W:8], a == 0, a == 7)
+            return ins
+        add("mx", "pe", f_x, ["zm0", key("s2")], [kP], 8 * cost["mm"])
+        add("xh", "dve", lambda: g.vector.tensor_scalar(small("xh"), P[:, 0:N2], -1.0, None, A.mult), [], [kP, key("xh")], plain(N2))
+
+        def f_prop():
+            x0, x1 = small("xh", 0, N2, 2), small("xh", 1, N2, 2)
+            g.tensor.matmul(P[:, N2:N2 + NC], mat(LO, 0), x0, True, False)
+            g.tensor.matmul(P[:, N2:N2 + NC], mat(LO, 8), x1, False, True)
+            g.tensor.matmul(P[:, N2 + NC:2 * N2], mat(HI, -8), x0, True, False)
+            return g.tensor.matmul(P[:, N2 + NC:2 * N2], mat(HI, 0), x1, False, True)
+        add("mprop", "pe", f_prop, ["pm0", "pm1", key("xh")], [kP], 4 * cost["mm"])
+        add("prop", "dve", lambda: g.vector.tensor_scalar(small("prop"), P[:, N2:2 * N2], 2048.0, None, A.add),
+            [], [kP, key("prop")], plain(N2))
+        add("old", "dve", lambda: g.vector.tensor_scalar(small("old"), bL, -1.0, 2048.0, A.mult, A.add), [kE, kF], [key("old")],
+            plain(N2, 0.5))
+
+        def f_d():
+            oE, oF = small("old", 0, NC), small("old", NC, N2)
+            d0, d1 = P[:, 2 * N2:3 * N2:2], P[:, 2 * N2 + 1:3 * N2:2]
+            g.tensor.matmul(P[:, 2 * N2:3 * N2], mat(ID, 0), small("xh"), True, False)
+            g.tensor.matmul(d0, mat(LO, 0), oE, False, False)
+            g.tensor.matmul(d0, mat(LO, 8), oF, False, False)
+            g.tensor.matmul(d1, mat(HI, -8), oE, False, False)
+            return g.tensor.matmul(d1, mat(HI, 0), oF, False, True)
+        add("md", "pe", f_d, ["pm0", "pm1", "pm2", key("xh"), key("old")], [kP], 5 * cost["mm"])
+        add("b1", "act", lambda: g.scalar.activation(buf("b1"), vt.indirect(small("prop", 0, NC)), F.Abs, bias=0.25),
+            ["vt", key("prop")], [key("b1")], gath(W))
+        add("b2", "dve", lambda: g.vector.tensor_tensor(buf("b2"), vt.indirect(small("prop", NC, N2)), buf("b1"), A.add),
+            ["vt", key("prop"), key("b1")], [key("b2")], gath(W))
+        add("b3", "act", lambda: g.scalar.activation(B, buf("b2"), F.Abs, bias=-16.0), [key("b2")], [kB], plain(W))
+        add("ne", "dve", lambda: g.vector.tensor_tensor(buf("ne"), B, buf("a3"), A.not_equal), [key("a3")], [kB, key("ne")], plain(W))
+
+        def f_cnt():
+            ins = None
+            for a in range(8):
+                ins = g.tensor.matmul(P[:, 3 * N2:4 * N2], rowsum(1, a), ne[:, w0 + a:w0 + W:8], a == 0, a == 7)
+            return ins
+        add("mcnt", "pe", f_cnt, ["zm1", key("ne")], [kP], 8 * cost["mm"])
+        add("ok", "dve", lambda: g.vector.tensor_scalar(small("ok"), P[:, 3 * N2:4 * N2], 1.0, None, A.min), [], [kP, key("ok")],
+            plain(N2))
+        add("m", "dve", lambda: g.vector.tensor_tensor(small("mm"), P[:, 2 * N2:3 * N2], small("ok"), A.mult),
+            [key("ok")], [kP, key("m")], plain(N2))
+        add("new", "dve", lambda: g.vector.tensor_tensor(small("new"), P[:, 0:N2], small("mm"), A.add),
+            [key("m")], [kP, key("new")], plain(N2))
+        n0 = 4 * N2
+
+        def f_move():
+            ins = None
+            for par in range(2):
+                x = [small("new", 2 * par + u, N2, 4) for u in range(2)]
+                rot = 16 * par
+                if r == RO - 1:
+                    plan = [(P[:, n0 + 2 * par + h:n0 + N2:4],
+                             [(LOP + h, 1 - h, 0), (LOP + h, 9 - h, 1), (HIP + h, -6 - h, 0), (FBP + h, -h, 1)]) for h in range(2)]
+                elif r % 2 == 0:
+                    plan = [(P[:, n0 + par:n0 + NC:2], [(HI, -8, 0), (HI, 0, 1)]),
+                            (P[:, n0 + NC + par:n0 + N2:2], [(FA, 0, 0), (LO, 6, 1)])]
+                else:
+                    plan = [(P[:, n0 + par:n0 + NC:2], [(HI, -6, 0), (FB, 0, 1)]),
+                            (P[:, n0 + NC + par:n0 + N2:2], [(LO, 0, 0), (LO, 8, 1)])]
+                for o, terms in plan:
+                    for j, (k, sh, u) in enumerate(terms):
+                        ins = g.tensor.matmul(o, mat(k, sh + rot), x[u], j == 0, j == len(terms) - 1)
+            return ins
+        mats = range(LOP, FBP + 2) if r == RO - 1 else (LO, HI, FA if r % 2 == 0 else FB)
+        add("mmove", "pe", f_move, ["pm%d" % k for k in mats] + [key("new")], [kP], (16 if r == RO - 1 else 8) * cost["mm"])
+        add("snd", "dve", lambda: g.vector.tensor_scalar(small("snd"), P[:, n0:n0 + N2], -1.0, 2048.0, A.mult, A.add), [], [kP, key("snd")],
+            plain(N2))
+        land = T["lst%d" % (r + 1)][:, l0:l0 + N2]
+        i = add("rem", "pool",
+                lambda: g.remote_dma(land, small("snd"), T.sem["arr%d_%d" % (r, c)], T.sem.sent, dst_addr[1], dst_addr[0], out_mask),
+                [key("snd")], [], cost["issue"], 0.0, ("remote", 0))
+        add("arr", "none", None, [], ["l%d_%d_0" % (r + 1, c), "l%d_%d_1" % (r + 1, c)], 0.0, cost["remote"],
+            ("arr%d_%d" % (r, c), n_in), after=[i])
+
+    def last_piece(c, c0, NC):
+        l0 = 2 * c0
+        L = T["lst%d" % RO]
+        kL = "l%d_%d_0" % (RO, c)
+        w0, w1 = 32 * c0, 32 * (c0 + NC)
+        ad = int(ACT_D * NC + 0.5)
+        wm = w0 + 32 * ad
+        vt = T.vt[:, :]
+
+        def key(nm):
+            return "%s_z_%d" % (nm, c0)
+        add("zs", "act", lambda: g.scalar.activation(T.sg[:, w0:w1], vt.indirect(L[:, l0:l0 + 2 * NC]), F.Sign), ["vt", kL],
+            [key("sg")], gath(32 * NC))
+        add("zd1", "dve", lambda: g.vector.tensor_scalar(T.dd[:, wm:w1], vt.indirect(L[:, l0 + 2 * ad:l0 + 2 * NC]), -16.0, None, A.add),
+            ["vt", kL], [key("d1")], gath(w1 - wm))
+        if ad:
+            add("zd0", "act", lambda: g.scalar.activation(T.dd[:, w0:wm], vt.indirect(L[:, l0:l0 + 2 * ad]), F.Identity, bias=-16.0),
+                ["vt", kL], [key("d0")], gath(wm - w0))
+        fx = T.fx[:, c0:c0 + NC]
+        add("zf", "dve", lambda: g.vector.tensor_scalar(fx, T.sg[:, w0 + 31:w1:32], -16.0, None, A.mult), [key("sg")], [key("fx")], plain(NC))
+        add("zf", "dve", lambda: g.vector.memset(T.sg[:, w0 + 31:w1:32], 0.0), [], [key("sg")], plain(NC))
+        add("zf", "dve", lambda: g.vector.tensor_tensor(T.dd[:, w0 + 31:w1:32], T.dd[:, w0 + 31:w1:32], fx, A.add),
+            [key("fx")], [key("d0"), key("d1")], plain(NC, 2.0))
+
+        def rev(b):
+            return b[:, w1 - 1::-1] if w0 == 0 else b[:, w1 - 1:w0 - 1:-1]
+        add("zscan", "dve", lambda: g.vector.tensor_tensor_scan(rev(T.hs), rev(T.sg), rev(T.dd), 0.0, A.mult, A.add),
+            [key("sg"), key("d0"), key("d1")], [key("hs")], plain(32 * NC, 0.5))
+        add("zyb", "act", lambda: g.scalar.activation(T.ybs[:, c0:c0 + NC], T.hs[:, w0:w1:32], F.Identity, bias=16.0),
+            [key("hs")], [key("yb")], plain(NC))
+        add("zob", "sync", lambda: g.sync.dma_start(T.yb[:, c0:c0 + NC], T.ybs[:, c0:c0 + NC]), [key("yb")], [], 400.0,
+            cost["dma"], ("outs", 0))
+
+    def last_chunk(c):
+        l0, l1 = 2 * C0[c], 2 * (C0[c] + CH[c])
+        add("zyc", "dve", lambda: g.vector.tensor_copy(T.ycs[:, l0:l1], T["lst%d" % RO][:, l0:l1]), ["l%d_%d_0" % (RO, c)],
+            ["yc%d" % c], plain(l1 - l0))
+        add("zoc", "sync", lambda: g.sync.dma_start(T.yc[:, l0:l1], T.ycs[:, l0:l1]), ["yc%d" % c], [], 400.0,
+            cost["dma"], ("outs", 0))
+        cuts = [C0[c] + CH[c] * k // FIN[c] for k in range(FIN[c] + 1)]
+        for k in range(FIN[c]):
+            last_piece(c, cuts[k], cuts[k + 1] - cuts[k])
+
+    for r in range(RO):
+        for c in range(len(CH)):
+            seq[0] = r * len(CH) + c
+            round_chunk(r, c)
+    for c in range(len(CH)):
+        seq[0] = RO * len(CH) + c
+        last_chunk(c)
+    return ops
+
+
+def rank_program(g, core, T, topo):
+    rank = T.rank_of(core)
+    if rank is None:
+        return
+    n = len(T.cores)
+    dst = T.cores[(rank + 3) % n]
+    src = T.cores[(rank - 3) % n]
+    out_mask = topo.mask(core, dst)
+    n_out = len(topo.engines(core, dst))
+    n_in = len(topo.engines(src, core))
+    ops = build(T, g, topo.addr(dst, core), out_mask, n_in, COST)
+    order = ORDER
+    queue = {"act": g.scalar, "dve": g.vector, "pe": g.tensor, "pool": g, "sync": g.sync}
+    count = {"act": 0, "dve": 0, "pe": 0, "pool": 0}
+    done = {}
+    seen = {}
+    outs = 0
+    sent = 0
+    for i in order:
+        o = ops[i]
+        e = o["eng"]
+        if e == "none":
+            done[i] = o["sem"]
+            continue
+        need = {}
+        for d in o["deps"]:
+            if e == "pe" and ops[d]["eng"] == "pe":
+                continue
+            s, val = done[d]
+            need[s] = max(need.get(s, 0), val)
+        for s in sorted(need):
+            if seen.get((e, s), 0) < need[s]:
+                queue[e].wait_ge(T.sem[s], need[s])
+                seen[(e, s)] = need[s]
+        ins = o["fn"]()
+        if o["sem"] is None:
+            count[e] += 1
+            ins.then_inc(T.sem["c_" + e], 1)
+            done[i] = ("c_" + e, count[e])
+        elif o["sem"][0] == "remote":
+            sent += n_out
+        else:
+            ins.then_inc(T.sem[o["sem"][0]], 16)
+            done[i] = o["sem"]
+            if o["sem"][0] == "outs":
+                outs += 16
+    for e in ("pool", "pe", "dve", "act"):
+        g.wait_ge(T.sem["c_" + e], count[e])
+    g.wait_ge(T.sem.sent, sent)
+    g.sync.wait_ge(T.sem.outs, outs)

@@ -1,11 +1,11 @@
+import math
 from concourse.mybir import AluOpType, ActivationFunctionType
 
 RO = 4
-CH = [32, 32, 32, 32]
-NP = 4
-FIN = [1, 1, 1, 2]
-ACT_D = 0.4
-ORDER = [0, 1, 4, 5, 2, 3, 7, 9, 10, 11, 12, 13, 14, 52, 15, 49, 50, 6, 8, 17, 16, 55, 51, 18, 19, 21, 20, 41, 23, 36, 53, 22, 33, 76, 31, 54, 34, 25, 24, 27, 43, 26, 29, 44, 47, 32, 42, 56, 30, 28, 45, 37, 62, 38, 39, 35, 46, 99, 40, 84, 63, 79, 64, 122, 102, 80, 69, 75, 81, 70, 82, 103, 83, 86, 48, 85, 77, 72, 98, 65, 107, 87, 57, 66, 78, 104, 67, 100, 105, 68, 88, 73, 106, 121, 58, 89, 59, 60, 125, 90, 109, 61, 91, 126, 101, 92, 93, 110, 94, 145, 95, 127, 96, 123, 111, 128, 108, 97, 129, 112, 132, 148, 113, 124, 114, 144, 115, 116, 133, 117, 149, 118, 134, 146, 119, 168, 71, 120, 130, 150, 135, 151, 131, 152, 136, 171, 155, 137, 167, 138, 153, 139, 156, 140, 154, 147, 172, 141, 169, 142, 157, 143, 191, 173, 158, 174, 175, 159, 194, 178, 160, 190, 161, 176, 162, 179, 163, 170, 195, 164, 192, 165, 180, 74, 214, 166, 196, 181, 197, 177, 198, 182, 217, 201, 183, 213, 199, 184, 185, 202, 186, 218, 193, 200, 187, 215, 188, 203, 189, 237, 219, 204, 220, 221, 205, 240, 224, 206, 236, 245, 207, 222, 208, 225, 209, 216, 241, 210, 238, 211, 226, 260, 212, 242, 227, 243, 223, 244, 228, 263, 247, 246, 229, 259, 264, 230, 268, 231, 248, 232, 239, 233, 261, 234, 249, 235, 283, 265, 250, 266, 267, 251, 286, 270, 269, 252, 282, 287, 253, 254, 271, 255, 262, 256, 284, 257, 272, 306, 258, 288, 273, 289, 290, 274, 309, 293, 275, 305, 291, 276, 277, 294, 278, 310, 285, 292, 279, 307, 280, 295, 281, 329, 311, 296, 312, 313, 297, 314, 316, 332, 315, 328, 298, 333, 299, 300, 317, 301, 308, 302, 334, 318, 303, 330, 335, 352, 304, 336, 319, 339, 355, 320, 351, 321, 356, 340, 331, 322, 337, 357, 323, 358, 353, 341, 324, 338, 375, 325, 359, 326, 342, 362, 378, 327, 343, 374, 344, 379, 363, 354, 345, 380, 346, 381, 376, 364, 347, 348, 365, 349, 398, 382, 406, 350, 383, 360, 385, 401, 361, 366, 397, 367, 402, 386, 384, 377, 368, 403, 369, 404, 399, 370, 387, 421, 405, 388, 371, 408, 389, 424, 372, 373, 420, 409, 425, 407, 400, 426, 390, 427, 391, 428, 392, 410, 422, 393, 431, 411, 423, 394, 412, 432, 395, 396, 429, 433, 413, 430, 414, 415, 416, 445, 434, 417, 435, 418, 436, 437, 419, 447, 438, 446, 439, 458, 448, 440, 457, 441, 456, 442, 450, 449, 443, 451, 444, 459, 467, 468, 460, 461, 465, 454, 462, 469, 455, 466, 470, 488, 478, 476, 471, 477, 472, 479, 463, 452, 480, 464, 481, 487, 473, 453, 483, 482, 474, 490, 489, 475, 484, 491, 485, 492, 486, 493, 494, 495]
+NCH, NC = 4, 32
+NP = 6
+SQ_ACT = (1, 3, 5, 7)
+LOADS = 4
 
 SCRATCH = {
     "vt": ("sbuf", [128, 4096], "bfloat16"),
@@ -17,6 +17,7 @@ SCRATCH = {
     "ones": ("sbuf", [128, 512], "bfloat16"),
     "sel": ("sbuf", [128, 1024], "bfloat16"),
     "zm": ("sbuf", [128, 2 * 144], "bfloat16"),
+    "zd": ("sbuf", [128, 2 * 144], "bfloat16"),
     "pm": ("sbuf", [128, 11 * 160], "bfloat16"),
     "mi": ("sbuf", [128, 64], "int32"),
     "mj": ("sbuf", [128, 64], "int32"),
@@ -24,30 +25,54 @@ SCRATCH = {
     "dd": ("sbuf", [128, 4096], "bfloat16"),
     "hs": ("sbuf", [128, 4096], "bfloat16"),
     "fx": ("sbuf", [128, 128], "bfloat16"),
+    "okb": ("sbuf", [128, 512], "bfloat16"),
     "ycs": ("sbuf", [128, 256], "float32"),
     "ybs": ("sbuf", [128, 128], "float32"),
 }
 for _r in range(RO + 1):
     SCRATCH["lst%d" % _r] = ("sbuf", [128, 256], "uint16")
 for _r in range(RO):
-    for _n in ("s1", "a1", "a2", "a3", "b1", "b2", "ne"):
+    for _n in ("s1", "a1", "a2", "a3", "b1", "b2", "b3"):
         SCRATCH["%s_%d" % (_n, _r)] = ("sbuf", [128, 2048], "bfloat16")
+    SCRATCH["ne_%d" % _r] = ("sbuf", [128, 1024], "bfloat16")
     SCRATCH["s2_%d" % _r] = ("sbuf", [128, 2048], "float16")
     SCRATCH["prop%d" % _r] = ("sbuf", [128, 256], "uint16")
     SCRATCH["snd%d" % _r] = ("sbuf", [128, 256], "uint16")
     SCRATCH["old%d" % _r] = ("sbuf", [128, 256], "float16")
     SCRATCH["xh%d" % _r] = ("sbuf", [128, 256], "float16")
-    SCRATCH["new%d" % _r] = ("sbuf", [128, 256], "float16")
-    SCRATCH["mm%d" % _r] = ("sbuf", [128, 256], "float32")
-    SCRATCH["ok%d" % _r] = ("sbuf", [128, 256], "float32")
+    SCRATCH["new%d" % _r] = ("sbuf", [128, 512], "float16")
 for _b in range(8):
     SCRATCH["ps%d" % _b] = ("psum", [128, 512], "float32")
 
 SEMAPHORES = ["c_act", "c_dve", "c_pe", "c_pool", "in_sq", "in_lp", "in_v", "outs", "sent"] + \
-    ["arr%d_%d" % (r, c) for r in range(RO) for c in range(len(CH))]
+    ["arr%d_%d" % (r, c) for r in range(RO) for c in range(NCH)]
 
-COST = {"g": 1.3, "f": 1.04, "fix": 55.0, "mm": 34.0, "hop": 80.0, "remote": 2600.0, "issue": 500.0, "dma": 2000.0,
-        "bw": 250.0}
+KEYS = ("f", "g", "mm", "fix", "pfix", "act", "same", "hop", "pehop", "wake", "issue", "remote", "first", "bw", "dma", "pool", "late")
+COSTS = [dict(zip(KEYS, c)) for c in (
+    (0.86, 1.0, 12, 139, 34, 44, 200, 82, 20, 763, 1147, 1211, 727, 335, 2247, 83, 162),
+    (0.88, 1.15, 12, 81, 41, 53, 169, 32, 226, 50, 909, 2288, 300, 490, 2215, 57, 682),
+    (0.99, 1.04, 14, 91, 0, 70, 200, 78, 119, 88, 1216, 1200, 3016, 407, 1730, 33, 213),
+    (0.85, 1.10, 12, 86, 8, 40, 0, 76, 171, 245, 261, 2836, 528, 322, 2332, 76, 1093),
+    (0.92, 1.10, 15, 100, 12, 40, 68, 198, 198, 222, 574, 2166, 1283, 370, 1324, 50, 500),
+    (1.16, 2.16, 17, 91, 20, 40, 174, 200, 200, 500, 765, 2250, 423, 250, 1500, 50, 500))]
+COST = COSTS[0]
+TURNS, HEAT, SEED = 20000, 0.0015, 3
+STAGE = {
+    "ld1": -9.0, "ld0": -9.0, "ld2": -8.9, "arr": -9, "mi": -8.0, "ones": -8.0, "sel0": -7.9, "sel1": -7.8, "mt0": -7.5,
+    "mt1": -7.4, "mt2": -7.3, "mt3": -7.2, "plo": -7.19, "zm": -6.56, "sqh": -6.53, "l0_1": -6.4, "l0_0": -6.3,
+    "sqm0": -2.91, "sqe0": -7.51, "sqm1": -3.26, "sqe1": -3.8, "sqm2": -5.76, "sqe2": -4.69, "sqm3": -2.52, "sqe3": -1.59,
+    "sqm4": -5.22, "sqe4": -3.85, "sqm5": -4.04, "sqe5": -7.32, "sqm6": 0.26, "sqe6": -2.34, "sqm7": -6.28, "sqe7": -5.1,
+    "pid": -4.57, "old0": -3.23, "phi": -3.06, "zd": -2.87, "w0": -2.77, "pfa": -2.25, "w1": -2.11, "okb": 0.3, "pfb": 4.84,
+    "pz": 9.92,
+    "s1": -1.43, "s2": -0.39, "mx": -0.55, "xh": -0.1, "mprop": -4.58, "prop": 0.39, "a1": -0.09, "old": 0.15, "md": -0.13,
+    "a2": 0.43, "a3": 0.63, "mpa3": 0.66, "b1": -2.14, "b2": 0.81, "mpb2": 1.22, "b3r": 1.32, "mpb3": -2.18, "ne": 0.87,
+    "mcnt": -0.56, "ok": 1.62, "new": 0.02, "mmove": -0.78, "snd": 1.86, "rem": 2.95,
+    "zyc": 0.31, "zoc": -0.42, "zs": 0.52, "zx": 0.73, "zf": 0.78, "zscan": 1.31, "zyb": -0.63, "zob": 2.86}
+SHIFT = {
+    ("s1", 0): -3.7, ("s2", 0): -3.08, ("xh", 0): -1.65, ("prop", 0): -0.31, ("b1", 0): 1.67, ("b2", 0): 0.02,
+    ("s1", 1): -0.95, ("s2", 1): -4.81, ("xh", 1): -2.8, ("prop", 1): -0.27, ("a1", 1): -0.19, ("s1", 2): -1.38,
+    ("s2", 2): -0.25, ("s1", 3): 0.5, ("s2", 3): -0.09, ("b3r", 14): 0.31, ("ne", 14): 0.59, ("ok", 14): 0.28,
+    ("snd", 14): 0.48, ("a2", 15): 0.28, ("b1", 15): -4.32, ("zscan", 18): 0.65, ("zs", 19): -0.58, ("zx", 19): -0.96}
 
 
 def build(T, g, dst_addr, out_mask, n_in, cost):
@@ -57,7 +82,7 @@ def build(T, g, dst_addr, out_mask, n_in, cost):
     last_w = {}
     readers = {}
     seq = [-1]
-    C0 = [sum(CH[:c]) for c in range(len(CH))]
+    C0 = [64 * (c % 2) + NC * (c // 2) for c in range(NCH)]
 
     def add(typ, eng, fn, reads, writes, dur, lat=0.0, sem=None, after=()):
         deps = set(after)
@@ -70,6 +95,8 @@ def build(T, g, dst_addr, out_mask, n_in, cost):
             deps.update(readers.get(k, ()))
         i = len(ops)
         deps.discard(i)
+        if sem is None:
+            dur += cost.get(eng, 0.0)
         for k in reads:
             readers.setdefault(k, []).append(i)
         for k in writes:
@@ -83,26 +110,33 @@ def build(T, g, dst_addr, out_mask, n_in, cost):
         return cost["fix"] + cost["g"] * n
 
     def plain(n, k=1.0):
-        return cost["fix"] * 0.3 + cost["f"] * max(64.0, k * n)
+        return cost["pfix"] + cost["f"] * max(64.0, k * n)
+
+    def mm(n):
+        return cost["mm"] + 0.5 * cost["f"] * max(64.0, n)
 
     def pool(n):
         return 170.0 + 2 * cost["f"] * n
 
-    def asel(typ, out, in_, pattern, op, base, cm, reads, writes, n):
-        add(typ, "pool", lambda: g.affine_select(out, in_, pattern, op, 0.0, base, cm), reads, writes, pool(n))
+    def load(n):
+        return cost["dma"] + n / cost["bw"]
+
+    def asel(typ, out, in_, pattern, op, base, cm, reads, writes, n, fill=0.0):
+        add(typ, "pool", lambda: g.affine_select(out, in_, pattern, op, fill, base, cm), reads, writes, pool(n))
 
     ps = [T["ps%d" % b] for b in range(8)]
-    add("ld0", "sync", lambda: g.sync.dma_start(T.sqi[:, :], T.sq[:, :]), [], ["sqi"], 100.0,
-        cost["dma"] + 262144 / cost["bw"], ("in_sq", 16))
+    vt = T.vt[:, :]
     add("ld1", "act", lambda: g.scalar.dma_start(T.lpi[0:128:2, 1:513], T.lp[:, :]), [], ["lpa"], 100.0,
-        cost["dma"] + 400000 / cost["bw"], ("in_lp", 32))
+        load(262144) + cost["late"], ("in_lp", 32))
     add("ld1", "act", lambda: g.scalar.dma_start(T.lpi[1:128:2, 0:512], T.lp[:, :]), [], ["lpb"], 100.0,
-        cost["dma"] + 520000 / cost["bw"], ("in_lp", 32))
-    add("ld2", "sync", lambda: g.sync.dma_start(T.vt[:, :], T.v[:, :]), [], ["vt"], 100.0,
-        cost["dma"] + 1570000 / cost["bw"], ("in_v", 16))
+        load(400000) + cost["late"], ("in_lp", 32))
+    add("ld0", "sync", lambda: g.sync.dma_start(T.sqi[:, :], T.sq[:, :]), [], ["sqi"], 100.0, load(310000), ("in_sq", 16))
+    add("ld2", "sync", lambda: g.sync.dma_start(T.vt[:, :], T.v[:, :]), [], ["vt"], 100.0, load(1570000), ("in_v", 16))
     add("mi", "pool", lambda: g.iota(T.mi[:, :], [[-1, 64]], 128, 1), [], ["mi"], pool(64))
     add("ones", "dve", lambda: g.vector.memset(T.ones[:, :], 1.0), [], ["ones"], plain(512, 0.5))
     add("zm", "dve", lambda: g.vector.memset(T.zm[:, :], 0.0), [], ["zm0", "zm1"], plain(288, 0.5))
+    add("zm", "dve", lambda: g.vector.memset(T.zd[:, :], 0.0), [], ["zd0", "zd1"], plain(288, 0.5))
+    add("okb", "dve", lambda: g.vector.memset(T.okb[:, :], 0.0), [], ["okb"], plain(512, 0.5))
     for hf in range(2):
         asel("sel%d" % hf, T.sel[:, 512 * hf:512 * hf + 512], T.ones[:, :], [[-1, 4], [0, 8], [-8, 16]], A.is_equal,
              -4 * hf, 1, ["ones"], ["sel%d" % hf], 512)
@@ -114,40 +148,51 @@ def build(T, g, dst_addr, out_mask, n_in, cost):
         add("mt0", "dve", lambda n=n: g.vector.tensor_copy(T.mt[:, n:2 * n], T.mt[:, 0:n]), ["mt0"], ["mt0"], plain(n, 0.5))
         n *= 2
     add("mt1", "act", lambda: g.scalar.activation(T.mt[:, 1024:2048], T.mt[:, 0:1024], F.Copy), ["mt0"], ["mt1"], plain(1024))
-    add("mt2", "act", lambda: g.scalar.activation(T.mt[:, 2048:3072], T.mt[:, 0:1024], F.Copy), ["mt0"], ["mt2"], plain(1024))
+    add("mt2", "dve", lambda: g.vector.tensor_copy(T.mt[:, 2048:3072], T.mt[:, 0:1024]), ["mt0"], ["mt2"], plain(1024, 0.5))
     add("mt3", "dve", lambda: g.vector.tensor_copy(T.mt[:, 3072:4096], T.mt[:, 0:1024]), ["mt0"], ["mt3"], plain(1024, 0.5))
     MT = ["mt0", "mt1", "mt2", "mt3"]
     add("sqh", "dve", lambda: g.vector.tensor_scalar(T.sqh[:, :], T.sqi[:, :], -2048.0, None, A.add), ["sqi"], ["sqh"],
         plain(512))
     for s in range(8):
         add("sqm%d" % s, "pe", lambda s=s: g.tensor.matmul(ps[s][:, :], T.sel[:, 128 * s:128 * s + 128], T.sqh[:, :], True, True),
-            ["sel%d" % (s // 4), "sqh"], ["ps%d" % s], 8 * cost["mm"])
-        if s % 2 == 0:
+            ["sel%d" % (s // 4), "sqh"], ["ps%d" % s], mm(512))
+        if s in SQ_ACT:
             add("sqe%d" % s, "act", lambda s=s: g.scalar.activation(T.sqt[:, 512 * s:512 * s + 512], ps[s][:, :], F.Copy),
                 [], ["ps%d" % s, "sqt%d" % s], plain(512))
         else:
             add("sqe%d" % s, "dve", lambda s=s: g.vector.tensor_copy(T.sqt[:, 512 * s:512 * s + 512], ps[s][:, :]),
                 [], ["ps%d" % s, "sqt%d" % s], plain(512))
     SQT = ["sqt%d" % s for s in range(8)]
-    for c, nc in enumerate(CH):
-        for b in range(2):
-            s0 = 1 + 256 * b + 2 * C0[c]
-            d0 = 2 * C0[c] + nc * b
-            add("l0_%d" % c, "dve", lambda nc=nc, d0=d0, s0=s0: g.vector.tensor_copy(
-                T.lst0[:, d0:d0 + nc], T.lpi[:, s0:s0 + 2 * nc - 1:2]),
-                ["lpa", "lpb"], ["l0_%d_%d" % (c, b)], plain(nc))
+    for b in (1, 0):
+        for u in range(2):
+            add("l0_%d" % b, "dve", lambda b=b, u=u: g.vector.tensor_copy(
+                T.lst0[:, 128 * b + 64 * u:128 * b + 64 * u + 64], T.lpi[:, 1 + 256 * b + 2 * u:256 + 256 * b:4]),
+                ["lpa", "lpb"], ["l0_%d" % b], plain(64))
+    add("old0", "dve", lambda: g.vector.tensor_scalar(T.old0[:, :], T.lst0[:, :], -1.0, 2048.0, A.mult, A.add), ["l0_0", "l0_1"],
+        ["old0"], plain(256, 0.5))
 
     for j, lo, hi in ((7, 0, 7), (15, 8, 15)):
         col = T.zm[:, j:128:16]
         asel("w0", col, T.ones[:, 0:8], [[-16, 8]], A.is_ge, -lo, 1, ["ones"], ["zm0"], 8)
         asel("w0", col, col, [[16, 8]], A.is_ge, hi, -1, [], ["zm0"], 8)
-    col = T.zm[:, 144 + 7:144 + 128:8]
-    asel("w1", col, T.ones[:, 0:16], [[-16, 8], [0, 2]], A.is_ge, 0, 1, ["ones"], ["zm1"], 16)
-    asel("w1", col, col, [[16, 8], [0, 2]], A.is_ge, 15, -1, [], ["zm1"], 16)
+    for j, lo, hi in ((6, 0, 7), (7, 8, 15)):
+        col = T.zm[:, 144 + j:144 + 128:8]
+        asel("w1", col, T.ones[:, 0:16], [[-16, 8], [0, 2]], A.is_ge, -lo, 1, ["ones"], ["zm1"], 16)
+        asel("w1", col, col, [[16, 8], [0, 2]], A.is_ge, hi, -1, [], ["zm1"], 16)
 
     def rowsum(k, a):
-        o = 144 * k + 7 - a
+        o = 144 * k + 7 - k - a
         return T.zm[:, o:o + 128]
+
+    z0 = T.zd[:, 8:136]
+    asel("zd", z0, z0, [[-16, 8], [-2, 16]], A.not_equal, 0, 1, [], ["zd0"], 128, 1.0)
+    asel("zd", z0, z0, [[-16, 8], [-2, 16]], A.not_equal, -1, 1, [], ["zd0"], 128, 64.0)
+    asel("zd", z0, z0, [[0, 8], [-1, 16]], A.is_ge, 7, 0, [], ["zd0"], 128)
+    add("zd", "dve", lambda: g.vector.tensor_scalar(T.zd[:, 152:280], z0, -2.0, None, A.mult), ["zd0"], ["zd1"], plain(128, 0.5))
+
+    def packer(k, half):
+        o = 144 * k + 8 - 8 * half
+        return T.zd[:, o:o + 128]
 
     LO, HI, ID, FA, FB, LOP, HIP, FBP = 0, 1, 2, 3, 4, 5, 7, 9
     base = {LO: 32, HI: 16, ID: 16, FA: 16, FB: 16, LOP: 32, LOP + 1: 32, HIP: 16, HIP + 1: 16, FBP: 16, FBP + 1: 16}
@@ -187,173 +232,274 @@ def build(T, g, dst_addr, out_mask, n_in, cost):
         for k, src in ((LOP, LO), (HIP, HI), (FBP, FB)):
             keep("pz", k + h, src, [[0, 80], [1, 2]], A.is_equal, -h)
 
+    W, N2 = 16 * NC, 2 * NC
+
     def round_chunk(r, c):
-        NC = CH[c]
-        W = 16 * NC
-        N2 = 2 * NC
-        L = T["lst%d" % r]
+        L, O, PR = T["lst%d" % r], T["old%d" % r], T["prop%d" % r]
         l0 = 2 * C0[c]
-        eL, fL, bL = L[:, l0:l0 + NC], L[:, l0 + NC:l0 + N2], L[:, l0:l0 + N2]
-        kE, kF = "l%d_%d_0" % (r, c), "l%d_%d_1" % (r, c)
-        w0 = 16 * C0[c]
+        e0, f0 = l0, l0 + NC
+        kE = kF = "l%d_%d" % (r, c)
+        kO = "old_%d_%d" % (r, c)
+        if r == 0:
+            e0, f0 = C0[c], 128 + C0[c]
+            kE, kF, kO = "l0_0", "l0_1", "old0"
+        eL, fL = L[:, e0:e0 + NC], L[:, f0:f0 + NC]
+        w0 = 8 * l0
 
-        def buf(nm, a=0, b=W):
-            return T["%s_%d" % (nm, r)][:, w0 + a:w0 + b]
+        def buf(nm, a=0, st=1):
+            return T["%s_%d" % (nm, r)][:, w0 + a:w0 + W:st]
 
-        def small(nm, a=0, b=N2, st=1):
-            return T["%s%d" % (nm, r)][:, l0 + a:l0 + b:st]
+        def small(nm, a=0, st=1):
+            return T["%s%d" % (nm, r)][:, l0 + a:l0 + N2:st]
 
         def key(nm):
             return "%s_%d_%d" % (nm, r, c)
-        bp = seq[0] % NP
-        bb = NP + seq[0] % (8 - NP)
-        P = ps[bp]
-        kP = "ps%d" % bp
-        B = ps[bb][:, 0:W]
-        kB = "ps%d" % bb
-        s2 = T["s2_%d" % r]
-        ne = T["ne_%d" % r]
-        vt = T.vt[:, :]
-        add("a1", "act", lambda: g.scalar.activation(buf("a1"), vt.indirect(eL), F.Abs, bias=0.25), ["vt", kE], [key("a1")], gath(W))
-        add("s1", "act", lambda: g.scalar.activation(buf("s1"), T.mt[:, :].indirect(fL), F.Copy), MT + [kF],
-            [key("s1")], gath(W))
-        add("a2", "dve", lambda: g.vector.tensor_tensor(buf("a2"), vt.indirect(fL), buf("a1"), A.add),
-            ["vt", kF, key("a1")], [key("a2")], gath(W))
-        add("a3", "act", lambda: g.scalar.activation(buf("a3"), buf("a2"), F.Abs, bias=-16.0), [key("a2")], [key("a3")],
-            plain(W))
-        add("s2", "dve", lambda: g.vector.tensor_tensor(buf("s2"), T.sqt[:, :].indirect(eL), buf("s1"), A.mult),
-            SQT + [kE, key("s1")], [key("s2")], gath(W))
+        bp, bb = seq[0] % NP, NP + seq[0] % (8 - NP)
+        P, kP, B, kB = ps[bp], "ps%d" % bp, ps[bb], "ps%d" % bb
+        X = P[:, 1:2 * N2:2]
+        ne, h0 = T["ne_%d" % r], w0 // 2
+
+        def pair(side, first, k1, win, lst, k2, op):
+            add(side + "1", "act", first, k1, [key(side + "1")], gath(W))
+            add(side + "2", "dve", lambda: g.vector.tensor_tensor(buf(side + "2"), win.indirect(lst), buf(side + "1"), op),
+                k2 + [key(side + "1")], [key(side + "2")], gath(W))
+        pair("s", lambda: g.scalar.activation(buf("s1"), T.mt[:, :].indirect(fL), F.Copy), MT + [kF],
+             T.sqt[:, :], eL, SQT + [kE], A.mult)
+        pair("a", lambda: g.scalar.activation(buf("a1"), vt.indirect(eL), F.Abs, bias=0.25), ["vt", kE], vt, fL, ["vt", kF], A.add)
+        add("a3", "act", lambda: g.scalar.activation(buf("a3"), buf("a2"), F.Abs, bias=-16.0), [key("a2")], [key("a3")], plain(W))
 
         def f_x():
             ins = None
             for a in range(8):
-                ins = g.tensor.matmul(P[:, 0:N2], rowsum(0, a), s2[:, w0 + a:w0 + W:8], a == 0, a == 7)
+                ins = g.tensor.matmul(X, rowsum(0, a), buf("s2", a, 8), a == 0, a == 7)
             return ins
-        add("mx", "pe", f_x, ["zm0", key("s2")], [kP], 8 * cost["mm"])
-        add("xh", "dve", lambda: g.vector.tensor_scalar(small("xh"), P[:, 0:N2], -1.0, None, A.mult), [], [kP, key("xh")], plain(N2))
+        add("mx", "pe", f_x, ["zm0", key("s2")], [kP], 8 * mm(N2))
+        add("xh", "dve", lambda: g.vector.tensor_scalar(small("xh"), X, -1.0, None, A.mult), [], [kP, key("xh")], plain(N2))
 
         def f_prop():
-            x0, x1 = small("xh", 0, N2, 2), small("xh", 1, N2, 2)
-            g.tensor.matmul(P[:, N2:N2 + NC], mat(LO, 0), x0, True, False)
-            g.tensor.matmul(P[:, N2:N2 + NC], mat(LO, 8), x1, False, True)
-            g.tensor.matmul(P[:, N2 + NC:2 * N2], mat(HI, -8), x0, True, False)
-            return g.tensor.matmul(P[:, N2 + NC:2 * N2], mat(HI, 0), x1, False, True)
-        add("mprop", "pe", f_prop, ["pm0", "pm1", key("xh")], [kP], 4 * cost["mm"])
-        add("prop", "dve", lambda: g.vector.tensor_scalar(small("prop"), P[:, N2:2 * N2], 2048.0, None, A.add),
+            x0, x1 = small("xh", 0, 2), small("xh", 1, 2)
+            g.tensor.matmul(P[:, 2 * N2:2 * N2 + NC], mat(LO, 0), x0, True, False)
+            g.tensor.matmul(P[:, 2 * N2:2 * N2 + NC], mat(LO, 8), x1, False, True)
+            g.tensor.matmul(P[:, 2 * N2 + NC:3 * N2], mat(HI, -8), x0, True, False)
+            return g.tensor.matmul(P[:, 2 * N2 + NC:3 * N2], mat(HI, 0), x1, False, True)
+        add("mprop", "pe", f_prop, ["pm0", "pm1", key("xh")], [kP], 4 * mm(NC))
+        add("prop", "dve", lambda: g.vector.tensor_scalar(small("prop"), P[:, 2 * N2:3 * N2], 2048.0, None, A.add),
             [], [kP, key("prop")], plain(N2))
-        add("old", "dve", lambda: g.vector.tensor_scalar(small("old"), bL, -1.0, 2048.0, A.mult, A.add), [kE, kF], [key("old")],
-            plain(N2, 0.5))
+        if r:
+            add("old", "dve", lambda: g.vector.tensor_scalar(small("old"), small("lst"), -1.0, 2048.0, A.mult, A.add), [kE], [kO],
+                plain(N2, 0.5))
 
         def f_d():
-            oE, oF = small("old", 0, NC), small("old", NC, N2)
-            d0, d1 = P[:, 2 * N2:3 * N2:2], P[:, 2 * N2 + 1:3 * N2:2]
-            g.tensor.matmul(P[:, 2 * N2:3 * N2], mat(ID, 0), small("xh"), True, False)
+            d0, d1 = P[:, 0:2 * N2:4], P[:, 2:2 * N2:4]
+            oE, oF = O[:, e0:e0 + NC], O[:, f0:f0 + NC]
+            g.tensor.matmul(P[:, 0:2 * N2:2], mat(ID, 0), small("xh"), True, False)
             g.tensor.matmul(d0, mat(LO, 0), oE, False, False)
             g.tensor.matmul(d0, mat(LO, 8), oF, False, False)
             g.tensor.matmul(d1, mat(HI, -8), oE, False, False)
             return g.tensor.matmul(d1, mat(HI, 0), oF, False, True)
-        add("md", "pe", f_d, ["pm0", "pm1", "pm2", key("xh"), key("old")], [kP], 5 * cost["mm"])
-        add("b1", "act", lambda: g.scalar.activation(buf("b1"), vt.indirect(small("prop", 0, NC)), F.Abs, bias=0.25),
-            ["vt", key("prop")], [key("b1")], gath(W))
-        add("b2", "dve", lambda: g.vector.tensor_tensor(buf("b2"), vt.indirect(small("prop", NC, N2)), buf("b1"), A.add),
-            ["vt", key("prop"), key("b1")], [key("b2")], gath(W))
-        add("b3", "act", lambda: g.scalar.activation(B, buf("b2"), F.Abs, bias=-16.0), [key("b2")], [kB], plain(W))
-        add("ne", "dve", lambda: g.vector.tensor_tensor(buf("ne"), B, buf("a3"), A.not_equal), [key("a3")], [kB, key("ne")], plain(W))
+        add("md", "pe", f_d, ["pm0", "pm1", "pm2", key("xh"), kO], [kP], 4 * mm(NC) + mm(N2))
+        pair("b", lambda: g.scalar.activation(buf("b1"), vt.indirect(PR[:, l0:l0 + NC]), F.Abs, bias=0.25), ["vt", key("prop")],
+             vt, PR[:, l0 + NC:l0 + N2], ["vt", key("prop")], A.add)
+        add("b3r", "dve", lambda: g.vector.tensor_scalar(buf("b3"), buf("b2"), 16.0, -8.0, A.max, A.add), [key("b2")], [key("b3")],
+            plain(W, 0.5))
+        for nm, k in (("a3", 0), ("b2", 0), ("b3", 1)):
+            def f_pack(nm=nm, k=k):
+                g.tensor.matmul(B[:, 0:4 * N2], packer(k, 0), buf(nm, 0, 2), nm == "a3", False)
+                return g.tensor.matmul(B[:, 0:4 * N2], packer(k, 1), buf(nm, 1, 2), False, nm == "b3")
+            add("mp" + nm, "pe", f_pack, ["zd%d" % k, key(nm)], [kB], 2 * mm(4 * N2))
+        add("ne", "act", lambda: g.scalar.activation(ne[:, h0:h0 + 4 * N2], B[:, 0:4 * N2], F.Abs), [], [kB, key("ne")], plain(4 * N2))
 
         def f_cnt():
             ins = None
-            for a in range(8):
-                ins = g.tensor.matmul(P[:, 3 * N2:4 * N2], rowsum(1, a), ne[:, w0 + a:w0 + W:8], a == 0, a == 7)
+            for b in range(4):
+                ins = g.tensor.matmul(P[:, 3 * N2:4 * N2], rowsum(1, 2 * b), ne[:, h0 + b:h0 + 4 * N2:4], b == 0, b == 3)
             return ins
-        add("mcnt", "pe", f_cnt, ["zm1", key("ne")], [kP], 8 * cost["mm"])
-        add("ok", "dve", lambda: g.vector.tensor_scalar(small("ok"), P[:, 3 * N2:4 * N2], 1.0, None, A.min), [], [kP, key("ok")],
-            plain(N2))
-        add("m", "dve", lambda: g.vector.tensor_tensor(small("mm"), P[:, 2 * N2:3 * N2], small("ok"), A.mult),
-            [key("ok")], [kP, key("m")], plain(N2))
-        add("new", "dve", lambda: g.vector.tensor_tensor(small("new"), P[:, 0:N2], small("mm"), A.add),
-            [key("m")], [kP, key("new")], plain(N2))
+        add("mcnt", "pe", f_cnt, ["zm1", key("ne")], [kP], 4 * mm(N2))
+        add("ok", "dve", lambda: g.vector.tensor_scalar(T.okb[:, 2 * l0 + 1:2 * (l0 + N2):2], P[:, 3 * N2:4 * N2], 0.0, None, A.is_gt),
+            ["okb"], [kP, "ok%d" % c], plain(N2))
+        new = T["new%d" % r]
+        add("new", "dve", lambda: g.vector.tensor_tensor_scan(new[:, 2 * l0:2 * (l0 + N2)], T.okb[:, 2 * l0:2 * (l0 + N2)],
+                                                              P[:, 0:2 * N2], 0.0, A.mult, A.add),
+            ["ok%d" % c], [kP, key("new")], plain(2 * N2))
         n0 = 4 * N2
 
         def f_move():
             ins = None
-            for par in range(2):
-                x = [small("new", 2 * par + u, N2, 4) for u in range(2)]
-                rot = 16 * par
-                if r == RO - 1:
-                    plan = [(P[:, n0 + 2 * par + h:n0 + N2:4],
-                             [(LOP + h, 1 - h, 0), (LOP + h, 9 - h, 1), (HIP + h, -6 - h, 0), (FBP + h, -h, 1)]) for h in range(2)]
-                elif r % 2 == 0:
-                    plan = [(P[:, n0 + par:n0 + NC:2], [(HI, -8, 0), (HI, 0, 1)]),
-                            (P[:, n0 + NC + par:n0 + N2:2], [(FA, 0, 0), (LO, 6, 1)])]
-                else:
-                    plan = [(P[:, n0 + par:n0 + NC:2], [(HI, -6, 0), (FB, 0, 1)]),
-                            (P[:, n0 + NC + par:n0 + N2:2], [(LO, 0, 0), (LO, 8, 1)])]
-                for o, terms in plan:
-                    for j, (k, sh, u) in enumerate(terms):
-                        ins = g.tensor.matmul(o, mat(k, sh + rot), x[u], j == 0, j == len(terms) - 1)
+            x = [new[:, 2 * (l0 + u) + 1:2 * (l0 + N2):4] for u in range(2)]
+            rot = 16 * (c % 2)
+            if r == RO - 1:
+                way = [(P[:, n0 + h:n0 + N2:2],
+                        [(LOP + h, 1 - h, 0), (LOP + h, 9 - h, 1), (HIP + h, -6 - h, 0), (FBP + h, -h, 1)]) for h in range(2)]
+            elif r % 2 == 0:
+                way = [(P[:, n0:n0 + NC], [(HI, -8, 0), (HI, 0, 1)]), (P[:, n0 + NC:n0 + N2], [(FA, 0, 0), (LO, 6, 1)])]
+            else:
+                way = [(P[:, n0:n0 + NC], [(HI, -6, 0), (FB, 0, 1)]), (P[:, n0 + NC:n0 + N2], [(LO, 0, 0), (LO, 8, 1)])]
+            for o, parts in way:
+                for j, (k, sh, u) in enumerate(parts):
+                    ins = g.tensor.matmul(o, mat(k, sh + rot), x[u], j == 0, j == len(parts) - 1)
             return ins
         mats = range(LOP, FBP + 2) if r == RO - 1 else (LO, HI, FA if r % 2 == 0 else FB)
-        add("mmove", "pe", f_move, ["pm%d" % k for k in mats] + [key("new")], [kP], (16 if r == RO - 1 else 8) * cost["mm"])
-        add("snd", "dve", lambda: g.vector.tensor_scalar(small("snd"), P[:, n0:n0 + N2], -1.0, 2048.0, A.mult, A.add), [], [kP, key("snd")],
-            plain(N2))
+        add("mmove", "pe", f_move, ["pm%d" % k for k in mats] + [key("new")], [kP], (8 if r == RO - 1 else 4) * mm(NC))
+        add("snd", "dve", lambda: g.vector.tensor_scalar(small("snd"), P[:, n0:n0 + N2], -1.0, 2048.0, A.mult, A.add), [],
+            [kP, key("snd")], plain(N2))
         land = T["lst%d" % (r + 1)][:, l0:l0 + N2]
         i = add("rem", "pool",
                 lambda: g.remote_dma(land, small("snd"), T.sem["arr%d_%d" % (r, c)], T.sem.sent, dst_addr[1], dst_addr[0], out_mask),
                 [key("snd")], [], cost["issue"], 0.0, ("remote", 0))
-        add("arr", "none", None, [], ["l%d_%d_0" % (r + 1, c), "l%d_%d_1" % (r + 1, c)], 0.0, cost["remote"],
+        add("arr", "none", None, [], ["l%d_%d" % (r + 1, c)], 0.0, cost["remote"] + (cost["first"] if seq[0] == 0 else 0.0),
             ("arr%d_%d" % (r, c), n_in), after=[i])
 
-    def last_piece(c, c0, NC):
-        l0 = 2 * c0
-        L = T["lst%d" % RO]
-        kL = "l%d_%d_0" % (RO, c)
+    def last_chunk(c):
+        c0 = C0[c]
+        l0, y0, y1 = 2 * c0, 2 * (c0 % 64), 2 * (c0 % 64 + NC)
         w0, w1 = 32 * c0, 32 * (c0 + NC)
-        ad = int(ACT_D * NC + 0.5)
-        wm = w0 + 32 * ad
-        vt = T.vt[:, :]
-
-        def key(nm):
-            return "%s_z_%d" % (nm, c0)
-        add("zs", "act", lambda: g.scalar.activation(T.sg[:, w0:w1], vt.indirect(L[:, l0:l0 + 2 * NC]), F.Sign), ["vt", kL],
-            [key("sg")], gath(32 * NC))
-        add("zd1", "dve", lambda: g.vector.tensor_scalar(T.dd[:, wm:w1], vt.indirect(L[:, l0 + 2 * ad:l0 + 2 * NC]), -16.0, None, A.add),
-            ["vt", kL], [key("d1")], gath(w1 - wm))
-        if ad:
-            add("zd0", "act", lambda: g.scalar.activation(T.dd[:, w0:wm], vt.indirect(L[:, l0:l0 + 2 * ad]), F.Identity, bias=-16.0),
-                ["vt", kL], [key("d0")], gath(wm - w0))
-        fx = T.fx[:, c0:c0 + NC]
-        add("zf", "dve", lambda: g.vector.tensor_scalar(fx, T.sg[:, w0 + 31:w1:32], -16.0, None, A.mult), [key("sg")], [key("fx")], plain(NC))
-        add("zf", "dve", lambda: g.vector.memset(T.sg[:, w0 + 31:w1:32], 0.0), [], [key("sg")], plain(NC))
+        L, kL = T["lst%d" % RO][:, l0:l0 + N2], "l%d_%d" % (RO, c)
+        for h in range(2):
+            add("zyc", "dve", lambda h=h: g.vector.tensor_copy(T.ycs[:, 2 * y0 + 2 * (c % 2) + h:2 * y1:4],
+                                                               T["lst%d" % RO][:, l0 + h:l0 + N2:2]),
+                [kL], ["yc%d_%d" % (c, h)], plain(NC))
+        if c % 2:
+            add("zoc", "sync", lambda: g.sync.dma_start(T.yc[:, 2 * y0:2 * y1], T.ycs[:, 2 * y0:2 * y1]),
+                ["yc%d_%d" % (k, h) for k in (c - 1, c) for h in range(2)], [], 400.0, cost["dma"], ("outs", 0))
+        sg, dd, fx = "sg%d" % c, "dd%d" % c, T.fx[:, c0:c0 + NC]
+        add("zs", "act", lambda: g.scalar.activation(T.sg[:, w0:w1], vt.indirect(L), F.Sign), ["vt", kL], [sg], gath(32 * NC))
+        add("zx", "dve", lambda: g.vector.tensor_scalar(T.dd[:, w0:w1], vt.indirect(L), -16.0, None, A.add), ["vt", kL], [dd],
+            gath(32 * NC))
+        add("zf", "act", lambda: g.scalar.activation(fx, T.sg[:, w0 + 31:w1:32], F.Identity, scale=-16.0), [sg], ["fx%d" % c], plain(NC))
+        add("zf", "dve", lambda: g.vector.memset(T.sg[:, w0 + 31:w1:32], 0.0), [], [sg], plain(NC))
         add("zf", "dve", lambda: g.vector.tensor_tensor(T.dd[:, w0 + 31:w1:32], T.dd[:, w0 + 31:w1:32], fx, A.add),
-            [key("fx")], [key("d0"), key("d1")], plain(NC, 2.0))
+            ["fx%d" % c], [dd], plain(NC, 2.0))
 
         def rev(b):
             return b[:, w1 - 1::-1] if w0 == 0 else b[:, w1 - 1:w0 - 1:-1]
         add("zscan", "dve", lambda: g.vector.tensor_tensor_scan(rev(T.hs), rev(T.sg), rev(T.dd), 0.0, A.mult, A.add),
-            [key("sg"), key("d0"), key("d1")], [key("hs")], plain(32 * NC, 0.5))
-        add("zyb", "act", lambda: g.scalar.activation(T.ybs[:, c0:c0 + NC], T.hs[:, w0:w1:32], F.Identity, bias=16.0),
-            [key("hs")], [key("yb")], plain(NC))
-        add("zob", "sync", lambda: g.sync.dma_start(T.yb[:, c0:c0 + NC], T.ybs[:, c0:c0 + NC]), [key("yb")], [], 400.0,
-            cost["dma"], ("outs", 0))
-
-    def last_chunk(c):
-        l0, l1 = 2 * C0[c], 2 * (C0[c] + CH[c])
-        add("zyc", "dve", lambda: g.vector.tensor_copy(T.ycs[:, l0:l1], T["lst%d" % RO][:, l0:l1]), ["l%d_%d_0" % (RO, c)],
-            ["yc%d" % c], plain(l1 - l0))
-        add("zoc", "sync", lambda: g.sync.dma_start(T.yc[:, l0:l1], T.ycs[:, l0:l1]), ["yc%d" % c], [], 400.0,
-            cost["dma"], ("outs", 0))
-        cuts = [C0[c] + CH[c] * k // FIN[c] for k in range(FIN[c] + 1)]
-        for k in range(FIN[c]):
-            last_piece(c, cuts[k], cuts[k + 1] - cuts[k])
+            [sg, dd], ["hs%d" % c], plain(32 * NC, 0.5))
+        add("zyb", "act", lambda: g.scalar.activation(T.ybs[:, y0 + c % 2:y1:2], T.hs[:, w0:w1:32], F.Identity, bias=16.0),
+            ["hs%d" % c], ["yb%d" % c], plain(NC))
+        if c % 2:
+            add("zob", "sync", lambda: g.sync.dma_start(T.yb[:, y0:y1], T.ybs[:, y0:y1]), ["yb%d" % (c - 1), "yb%d" % c], [],
+                400.0, cost["dma"], ("outs", 0))
 
     for r in range(RO):
-        for c in range(len(CH)):
-            seq[0] = r * len(CH) + c
+        for c in range(NCH):
+            seq[0] = r * NCH + c
             round_chunk(r, c)
-    for c in range(len(CH)):
-        seq[0] = RO * len(CH) + c
+    for c in range(NCH):
+        seq[0] = RO * NCH + c
         last_chunk(c)
     return ops
+
+
+def run_through(order, eng, deps, dur, lat):
+    free, last = [0.0] * 6, [-1] * 6
+    end, pred, queued = [0.0] * len(dur), [-1] * len(dur), [False] * len(dur)
+    for i in order:
+        e = eng[i]
+        t, p, q = free[e], last[e], True
+        for d, hop in deps[i]:
+            if end[d] + hop > t:
+                t, p, q = end[d] + hop, d, False
+        pred[i], queued[i] = p, q
+        if e != 5:
+            free[e], last[e] = t + dur[i], i
+        end[i] = t + dur[i] + lat[i]
+    total = max(end)
+    i, pairs = end.index(total), []
+    while pred[i] >= 0:
+        if queued[i]:
+            pairs.append((pred[i], i))
+        i = pred[i]
+    return total, pairs
+
+
+def plan(steps, costs):
+    ops = steps[0]
+    n = len(ops)
+    rank = []
+    for i, o in enumerate(ops):
+        own = max(o["seq"], 0) + STAGE[o["typ"]] + SHIFT.get((o["typ"], o["seq"]), 0.0) + 1e-5 * i
+        rank.append(max([own] + [rank[d] + 1e-5 for d in o["deps"]]))
+    order = sorted(range(n), key=lambda i: rank[i])
+    eng = [["act", "dve", "pe", "pool", "sync", "none"].index(o["eng"]) for o in ops]
+    users = [set() for _ in ops]
+    for i, o in enumerate(ops):
+        for d in o["deps"]:
+            users[d].add(i)
+
+    def wait(i, d, c):
+        if eng[i] == 5 or eng[i] == eng[d] == 2:
+            return 0.0
+        return c["wake"] if eng[d] == 5 or d < LOADS else c["same"] if eng[i] == eng[d] else c["pehop"] if eng[d] == 2 else c["hop"]
+    data = [([[(d, wait(i, d, c)) for d in o["deps"]] for i, o in enumerate(s)],
+             [o["dur"] for o in s], [o["lat"] for o in s]) for s, c in zip(steps, costs)]
+    seed = [SEED]
+
+    def draw():
+        seed[0] = (seed[0] * 6364136223846793005 + 1442695040888963407) % 2 ** 64
+        return (seed[0] >> 11) / 2.0 ** 53
+
+    def score(o):
+        runs = [run_through(o, eng, *d) for d in data]
+        return sum(math.log(r[0]) for r in runs) / len(runs), runs
+    now, runs = score(order)
+    best = (now, order)
+    for turn in range(TURNS):
+        pairs = runs[int(draw() * len(runs))][1]
+        if not pairs:
+            continue
+        u, v = pairs[int(draw() * len(pairs))]
+        a = order.index(u)
+        if draw() < 0.3:
+            a = max([k for k in range(a) if eng[order[k]] == eng[u]] or [a])
+        b = order.index(v)
+        need = {v}
+        for x in order[b - 1:a - 1 if a else None:-1]:
+            if users[x] & need:
+                need.add(x)
+        if order[a] in need:
+            continue
+        part = order[a:b + 1]
+        trial = order[:a] + [x for x in part if x in need] + [x for x in part if x not in need] + order[b + 1:]
+        loads = [x for x in trial[:b + 1] if x < LOADS]
+        if loads != list(range(len(loads))):
+            continue
+        s, r = score(trial)
+        if s <= now or draw() < math.exp((now - s) / (HEAT * (1 - turn / TURNS) + 1e-6)):
+            order, now, runs = trial, s, r
+            if s < best[0]:
+                best = (s, order)
+    return best[1]
+
+
+def waits(ops, order):
+    count = {"act": 0, "dve": 0, "pe": 0, "pool": 0}
+    place = {i: k for k, i in enumerate(order)}
+    done, knew, seen, need = {}, {}, {}, {}
+    for i in order:
+        o = ops[i]
+        e = o["eng"]
+        need[i] = []
+        if e == "none":
+            done[i], knew[i] = o["sem"], {}
+            continue
+        known = seen.setdefault(e, {})
+        for d in sorted(o["deps"], key=lambda d: -place[d]):
+            s, val = done[d]
+            if not (e == "pe" and ops[d]["eng"] == "pe") and known.get(s, 0) < val:
+                need[i].append((s, val))
+                known[s] = val
+                for k, w in knew[d].items():
+                    known[k] = max(known.get(k, 0), w)
+        knew[i] = dict(known)
+        if o["sem"] is None:
+            count[e] += 1
+            done[i] = ("c_" + e, count[e])
+        else:
+            done[i] = o["sem"]
+    return need, count
+
+
+PLAN = []
 
 
 def rank_program(g, core, T, topo):
@@ -366,40 +512,28 @@ def rank_program(g, core, T, topo):
     out_mask = topo.mask(core, dst)
     n_out = len(topo.engines(core, dst))
     n_in = len(topo.engines(src, core))
-    ops = build(T, g, topo.addr(dst, core), out_mask, n_in, COST)
-    order = ORDER
+    steps = [build(T, g, topo.addr(dst, core), out_mask, n_in, c) for c in COSTS]
+    if not PLAN:
+        PLAN.extend(plan(steps, COSTS))
+    ops = steps[0]
+    need, count = waits(ops, PLAN)
     queue = {"act": g.scalar, "dve": g.vector, "pe": g.tensor, "pool": g, "sync": g.sync}
-    count = {"act": 0, "dve": 0, "pe": 0, "pool": 0}
-    done = {}
-    seen = {}
     outs = 0
     sent = 0
-    for i in order:
+    for i in PLAN:
         o = ops[i]
         e = o["eng"]
         if e == "none":
-            done[i] = o["sem"]
             continue
-        need = {}
-        for d in o["deps"]:
-            if e == "pe" and ops[d]["eng"] == "pe":
-                continue
-            s, val = done[d]
-            need[s] = max(need.get(s, 0), val)
-        for s in sorted(need):
-            if seen.get((e, s), 0) < need[s]:
-                queue[e].wait_ge(T.sem[s], need[s])
-                seen[(e, s)] = need[s]
+        for s, val in need[i]:
+            queue[e].wait_ge(T.sem[s], val)
         ins = o["fn"]()
         if o["sem"] is None:
-            count[e] += 1
             ins.then_inc(T.sem["c_" + e], 1)
-            done[i] = ("c_" + e, count[e])
         elif o["sem"][0] == "remote":
             sent += n_out
         else:
             ins.then_inc(T.sem[o["sem"][0]], 16)
-            done[i] = o["sem"]
             if o["sem"][0] == "outs":
                 outs += 16
     for e in ("pool", "pe", "dve", "act"):

import math
from concourse.mybir import AluOpType, ActivationFunctionType

RO = 4
NCH, NC = 4, 32
NP = 6
SQ_ACT = (1, 3, 5, 7)
LOADS = 4

SCRATCH = {
    "vt": ("sbuf", [128, 4096], "bfloat16"),
    "mt": ("sbuf", [128, 4096], "bfloat16"),
    "sqt": ("sbuf", [128, 4096], "float32"),
    "sqi": ("sbuf", [128, 512], "int32"),
    "sqh": ("sbuf", [128, 512], "float16"),
    "lpi": ("sbuf", [128, 520], "int32"),
    "ones": ("sbuf", [128, 512], "bfloat16"),
    "sel": ("sbuf", [128, 1024], "bfloat16"),
    "zm": ("sbuf", [128, 2 * 144], "bfloat16"),
    "zd": ("sbuf", [128, 2 * 144], "bfloat16"),
    "pm": ("sbuf", [128, 11 * 160], "bfloat16"),
    "mi": ("sbuf", [128, 64], "int32"),
    "mj": ("sbuf", [128, 64], "int32"),
    "sg": ("sbuf", [128, 4096], "bfloat16"),
    "dd": ("sbuf", [128, 4096], "bfloat16"),
    "hs": ("sbuf", [128, 4096], "bfloat16"),
    "fx": ("sbuf", [128, 128], "bfloat16"),
    "okb": ("sbuf", [128, 512], "bfloat16"),
    "ycs": ("sbuf", [128, 256], "float32"),
    "ybs": ("sbuf", [128, 128], "float32"),
}
for _r in range(RO + 1):
    SCRATCH["lst%d" % _r] = ("sbuf", [128, 256], "uint16")
for _r in range(RO):
    for _n in ("s1", "a1", "a2", "a3", "b1", "b2", "b3"):
        SCRATCH["%s_%d" % (_n, _r)] = ("sbuf", [128, 2048], "bfloat16")
    SCRATCH["ne_%d" % _r] = ("sbuf", [128, 1024], "bfloat16")
    SCRATCH["s2_%d" % _r] = ("sbuf", [128, 2048], "float16")
    SCRATCH["prop%d" % _r] = ("sbuf", [128, 256], "uint16")
    SCRATCH["snd%d" % _r] = ("sbuf", [128, 256], "uint16")
    SCRATCH["old%d" % _r] = ("sbuf", [128, 256], "float16")
    SCRATCH["xh%d" % _r] = ("sbuf", [128, 256], "float16")
    SCRATCH["new%d" % _r] = ("sbuf", [128, 512], "float16")
for _b in range(8):
    SCRATCH["ps%d" % _b] = ("psum", [128, 512], "float32")

SEMAPHORES = ["c_act", "c_dve", "c_pe", "c_pool", "in_sq", "in_lp", "in_v", "outs", "sent"] + \
    ["arr%d_%d" % (r, c) for r in range(RO) for c in range(NCH)]

KEYS = ("f", "g", "mm", "fix", "pfix", "act", "same", "hop", "pehop", "wake", "issue", "remote", "first", "bw", "dma", "pool", "late")
COSTS = [dict(zip(KEYS, c)) for c in (
    (0.86, 1.0, 12, 139, 34, 44, 200, 82, 20, 763, 1147, 1211, 727, 335, 2247, 83, 162),
    (0.88, 1.15, 12, 81, 41, 53, 169, 32, 226, 50, 909, 2288, 300, 490, 2215, 57, 682),
    (0.99, 1.04, 14, 91, 0, 70, 200, 78, 119, 88, 1216, 1200, 3016, 407, 1730, 33, 213),
    (0.85, 1.10, 12, 86, 8, 40, 0, 76, 171, 245, 261, 2836, 528, 322, 2332, 76, 1093),
    (0.92, 1.10, 15, 100, 12, 40, 68, 198, 198, 222, 574, 2166, 1283, 370, 1324, 50, 500),
    (1.16, 2.16, 17, 91, 20, 40, 174, 200, 200, 500, 765, 2250, 423, 250, 1500, 50, 500))]
COST = COSTS[0]
TURNS, HEAT, SEED = 20000, 0.0015, 3
STAGE = {
    "ld1": -9.0, "ld0": -9.0, "ld2": -8.9, "arr": -9, "mi": -8.0, "ones": -8.0, "sel0": -7.9, "sel1": -7.8, "mt0": -7.5,
    "mt1": -7.4, "mt2": -7.3, "mt3": -7.2, "plo": -7.19, "zm": -6.56, "sqh": -6.53, "l0_1": -6.4, "l0_0": -6.3,
    "sqm0": -2.91, "sqe0": -7.51, "sqm1": -3.26, "sqe1": -3.8, "sqm2": -5.76, "sqe2": -4.69, "sqm3": -2.52, "sqe3": -1.59,
    "sqm4": -5.22, "sqe4": -3.85, "sqm5": -4.04, "sqe5": -7.32, "sqm6": 0.26, "sqe6": -2.34, "sqm7": -6.28, "sqe7": -5.1,
    "pid": -4.57, "old0": -3.23, "phi": -3.06, "zd": -2.87, "w0": -2.77, "pfa": -2.25, "w1": -2.11, "okb": 0.3, "pfb": 4.84,
    "pz": 9.92,
    "s1": -1.43, "s2": -0.39, "mx": -0.55, "xh": -0.1, "mprop": -4.58, "prop": 0.39, "a1": -0.09, "old": 0.15, "md": -0.13,
    "a2": 0.43, "a3": 0.63, "mpa3": 0.66, "b1": -2.14, "b2": 0.81, "mpb2": 1.22, "b3r": 1.32, "mpb3": -2.18, "ne": 0.87,
    "mcnt": -0.56, "ok": 1.62, "new": 0.02, "mmove": -0.78, "snd": 1.86, "rem": 2.95,
    "zyc": 0.31, "zoc": -0.42, "zs": 0.52, "zx": 0.73, "zf": 0.78, "zscan": 1.31, "zyb": -0.63, "zob": 2.86}
SHIFT = {
    ("s1", 0): -3.7, ("s2", 0): -3.08, ("xh", 0): -1.65, ("prop", 0): -0.31, ("b1", 0): 1.67, ("b2", 0): 0.02,
    ("s1", 1): -0.95, ("s2", 1): -4.81, ("xh", 1): -2.8, ("prop", 1): -0.27, ("a1", 1): -0.19, ("s1", 2): -1.38,
    ("s2", 2): -0.25, ("s1", 3): 0.5, ("s2", 3): -0.09, ("b3r", 14): 0.31, ("ne", 14): 0.59, ("ok", 14): 0.28,
    ("snd", 14): 0.48, ("a2", 15): 0.28, ("b1", 15): -4.32, ("zscan", 18): 0.65, ("zs", 19): -0.58, ("zx", 19): -0.96}


def build(T, g, dst_addr, out_mask, n_in, cost):
    A = AluOpType
    F = ActivationFunctionType
    ops = []
    last_w = {}
    readers = {}
    seq = [-1]
    C0 = [64 * (c % 2) + NC * (c // 2) for c in range(NCH)]

    def add(typ, eng, fn, reads, writes, dur, lat=0.0, sem=None, after=()):
        deps = set(after)
        for k in reads:
            if k in last_w:
                deps.add(last_w[k])
        for k in writes:
            if k in last_w:
                deps.add(last_w[k])
            deps.update(readers.get(k, ()))
        i = len(ops)
        deps.discard(i)
        if sem is None:
            dur += cost.get(eng, 0.0)
        for k in reads:
            readers.setdefault(k, []).append(i)
        for k in writes:
            last_w[k] = i
            readers[k] = []
        ops.append({"eng": eng, "fn": fn, "deps": sorted(deps), "dur": dur, "lat": lat, "sem": sem, "seq": seq[0],
                    "typ": typ})
        return i

    def gath(n):
        return cost["fix"] + cost["g"] * n

    def plain(n, k=1.0):
        return cost["pfix"] + cost["f"] * max(64.0, k * n)

    def mm(n):
        return cost["mm"] + 0.5 * cost["f"] * max(64.0, n)

    def pool(n):
        return 170.0 + 2 * cost["f"] * n

    def load(n):
        return cost["dma"] + n / cost["bw"]

    def asel(typ, out, in_, pattern, op, base, cm, reads, writes, n, fill=0.0):
        add(typ, "pool", lambda: g.affine_select(out, in_, pattern, op, fill, base, cm), reads, writes, pool(n))

    ps = [T["ps%d" % b] for b in range(8)]
    vt = T.vt[:, :]
    add("ld1", "act", lambda: g.scalar.dma_start(T.lpi[0:128:2, 1:513], T.lp[:, :]), [], ["lpa"], 100.0,
        load(262144) + cost["late"], ("in_lp", 32))
    add("ld1", "act", lambda: g.scalar.dma_start(T.lpi[1:128:2, 0:512], T.lp[:, :]), [], ["lpb"], 100.0,
        load(400000) + cost["late"], ("in_lp", 32))
    add("ld0", "sync", lambda: g.sync.dma_start(T.sqi[:, :], T.sq[:, :]), [], ["sqi"], 100.0, load(310000), ("in_sq", 16))
    add("ld2", "sync", lambda: g.sync.dma_start(T.vt[:, :], T.v[:, :]), [], ["vt"], 100.0, load(1570000), ("in_v", 16))
    add("mi", "pool", lambda: g.iota(T.mi[:, :], [[-1, 64]], 128, 1), [], ["mi"], pool(64))
    add("ones", "dve", lambda: g.vector.memset(T.ones[:, :], 1.0), [], ["ones"], plain(512, 0.5))
    add("zm", "dve", lambda: g.vector.memset(T.zm[:, :], 0.0), [], ["zm0", "zm1"], plain(288, 0.5))
    add("zm", "dve", lambda: g.vector.memset(T.zd[:, :], 0.0), [], ["zd0", "zd1"], plain(288, 0.5))
    add("okb", "dve", lambda: g.vector.memset(T.okb[:, :], 0.0), [], ["okb"], plain(512, 0.5))
    for hf in range(2):
        asel("sel%d" % hf, T.sel[:, 512 * hf:512 * hf + 512], T.ones[:, :], [[-1, 4], [0, 8], [-8, 16]], A.is_equal,
             -4 * hf, 1, ["ones"], ["sel%d" % hf], 512)
    add("mt0", "dve", lambda: g.vector.tensor_scalar(T.mj[:, :], T.mi[:, :], 7, None, A.bitwise_and), ["mi"], ["mj"], plain(64))
    add("mt0", "dve", lambda: g.vector.tensor_scalar(T.mt[:, 0:64], T.mj[:, :], 0.0, -1.0, A.is_equal, A.mult), ["mj"], ["mt0"],
        plain(64))
    n = 64
    while n < 1024:
        add("mt0", "dve", lambda n=n: g.vector.tensor_copy(T.mt[:, n:2 * n], T.mt[:, 0:n]), ["mt0"], ["mt0"], plain(n, 0.5))
        n *= 2
    add("mt1", "act", lambda: g.scalar.activation(T.mt[:, 1024:2048], T.mt[:, 0:1024], F.Copy), ["mt0"], ["mt1"], plain(1024))
    add("mt2", "dve", lambda: g.vector.tensor_copy(T.mt[:, 2048:3072], T.mt[:, 0:1024]), ["mt0"], ["mt2"], plain(1024, 0.5))
    add("mt3", "dve", lambda: g.vector.tensor_copy(T.mt[:, 3072:4096], T.mt[:, 0:1024]), ["mt0"], ["mt3"], plain(1024, 0.5))
    MT = ["mt0", "mt1", "mt2", "mt3"]
    add("sqh", "dve", lambda: g.vector.tensor_scalar(T.sqh[:, :], T.sqi[:, :], -2048.0, None, A.add), ["sqi"], ["sqh"],
        plain(512))
    for s in range(8):
        add("sqm%d" % s, "pe", lambda s=s: g.tensor.matmul(ps[s][:, :], T.sel[:, 128 * s:128 * s + 128], T.sqh[:, :], True, True),
            ["sel%d" % (s // 4), "sqh"], ["ps%d" % s], mm(512))
        if s in SQ_ACT:
            add("sqe%d" % s, "act", lambda s=s: g.scalar.activation(T.sqt[:, 512 * s:512 * s + 512], ps[s][:, :], F.Copy),
                [], ["ps%d" % s, "sqt%d" % s], plain(512))
        else:
            add("sqe%d" % s, "dve", lambda s=s: g.vector.tensor_copy(T.sqt[:, 512 * s:512 * s + 512], ps[s][:, :]),
                [], ["ps%d" % s, "sqt%d" % s], plain(512))
    SQT = ["sqt%d" % s for s in range(8)]
    for b in (1, 0):
        for u in range(2):
            add("l0_%d" % b, "dve", lambda b=b, u=u: g.vector.tensor_copy(
                T.lst0[:, 128 * b + 64 * u:128 * b + 64 * u + 64], T.lpi[:, 1 + 256 * b + 2 * u:256 + 256 * b:4]),
                ["lpa", "lpb"], ["l0_%d" % b], plain(64))
    add("old0", "dve", lambda: g.vector.tensor_scalar(T.old0[:, :], T.lst0[:, :], -1.0, 2048.0, A.mult, A.add), ["l0_0", "l0_1"],
        ["old0"], plain(256, 0.5))

    for j, lo, hi in ((7, 0, 7), (15, 8, 15)):
        col = T.zm[:, j:128:16]
        asel("w0", col, T.ones[:, 0:8], [[-16, 8]], A.is_ge, -lo, 1, ["ones"], ["zm0"], 8)
        asel("w0", col, col, [[16, 8]], A.is_ge, hi, -1, [], ["zm0"], 8)
    for j, lo, hi in ((6, 0, 7), (7, 8, 15)):
        col = T.zm[:, 144 + j:144 + 128:8]
        asel("w1", col, T.ones[:, 0:16], [[-16, 8], [0, 2]], A.is_ge, -lo, 1, ["ones"], ["zm1"], 16)
        asel("w1", col, col, [[16, 8], [0, 2]], A.is_ge, hi, -1, [], ["zm1"], 16)

    def rowsum(k, a):
        o = 144 * k + 7 - k - a
        return T.zm[:, o:o + 128]

    z0 = T.zd[:, 8:136]
    asel("zd", z0, z0, [[-16, 8], [-2, 16]], A.not_equal, 0, 1, [], ["zd0"], 128, 1.0)
    asel("zd", z0, z0, [[-16, 8], [-2, 16]], A.not_equal, -1, 1, [], ["zd0"], 128, 64.0)
    asel("zd", z0, z0, [[0, 8], [-1, 16]], A.is_ge, 7, 0, [], ["zd0"], 128)
    add("zd", "dve", lambda: g.vector.tensor_scalar(T.zd[:, 152:280], z0, -2.0, None, A.mult), ["zd0"], ["zd1"], plain(128, 0.5))

    def packer(k, half):
        o = 144 * k + 8 - 8 * half
        return T.zd[:, o:o + 128]

    LO, HI, ID, FA, FB, LOP, HIP, FBP = 0, 1, 2, 3, 4, 5, 7, 9
    base = {LO: 32, HI: 16, ID: 16, FA: 16, FB: 16, LOP: 32, LOP + 1: 32, HIP: 16, HIP + 1: 16, FBP: 16, FBP + 1: 16}

    def mat(k, shift):
        o = 160 * k + base[k] - shift
        return T.pm[:, o:o + 128]

    def diag(typ, k, d):
        o, b = 160 * k, base[k]
        kk = ["pm%d" % k]
        asel(typ, T.pm[:, o:o + b], T.ones[:, 0:b], [[-1, b]], A.is_equal, b - 128 - d, 1, ["ones"], kk, b)
        asel(typ, T.pm[:, o + b:o + 160], T.ones[:, 0:160 - b], [[-1, 160 - b]], A.is_equal, -d, 1, ["ones"], kk, 160 - b)

    def keep(typ, k, src, pattern, op, bs):
        asel(typ, T.pm[:, 160 * k:160 * k + 160], T.pm[:, 160 * src:160 * src + 160], pattern, op, bs, 0,
             ["pm%d" % src], ["pm%d" % k], 160)

    def column(typ, k, d, s):
        o = 160 * k
        kk = ["pm%d" % k]
        asel(typ, T.pm[:, o + 16 + d:o + 144:16], T.ones[:, 0:8], [[-16, 8]], A.is_equal, -s, 1, ["ones"], kk, 8)
        asel(typ, T.pm[:, o + d:o + d + 1], T.ones[:, 0:1], [[0, 1]], A.is_equal, -112 - s, 1, ["ones"], kk, 1)
    diag("plo", LO, 0)
    keep("plo", LO, LO, [[0, 10], [-1, 16]], A.is_ge, 7)
    diag("pid", ID, 0)
    keep("phi", HI, ID, [[0, 10], [1, 16]], A.is_ge, -8)
    diag("pfa", FA, 2)
    keep("pfa", FA, FA, [[0, 10], [-1, 16]], A.is_ge, 5)
    column("pfa", FA, 14, 1)
    column("pfa", FA, 15, 0)
    diag("pfb", FB, -2)
    keep("pfb", FB, FB, [[0, 10], [1, 16]], A.is_ge, -10)
    column("pfb", FB, 1, 14)
    column("pfb", FB, 0, 15)
    for h in range(2):
        for k, src in ((LOP, LO), (HIP, HI), (FBP, FB)):
            keep("pz", k + h, src, [[0, 80], [1, 2]], A.is_equal, -h)

    W, N2 = 16 * NC, 2 * NC

    def round_chunk(r, c):
        L, O, PR = T["lst%d" % r], T["old%d" % r], T["prop%d" % r]
        l0 = 2 * C0[c]
        e0, f0 = l0, l0 + NC
        kE = kF = "l%d_%d" % (r, c)
        kO = "old_%d_%d" % (r, c)
        if r == 0:
            e0, f0 = C0[c], 128 + C0[c]
            kE, kF, kO = "l0_0", "l0_1", "old0"
        eL, fL = L[:, e0:e0 + NC], L[:, f0:f0 + NC]
        w0 = 8 * l0

        def buf(nm, a=0, st=1):
            return T["%s_%d" % (nm, r)][:, w0 + a:w0 + W:st]

        def small(nm, a=0, st=1):
            return T["%s%d" % (nm, r)][:, l0 + a:l0 + N2:st]

        def key(nm):
            return "%s_%d_%d" % (nm, r, c)
        bp, bb = seq[0] % NP, NP + seq[0] % (8 - NP)
        P, kP, B, kB = ps[bp], "ps%d" % bp, ps[bb], "ps%d" % bb
        X = P[:, 1:2 * N2:2]
        ne, h0 = T["ne_%d" % r], w0 // 2

        def pair(side, first, k1, win, lst, k2, op):
            add(side + "1", "act", first, k1, [key(side + "1")], gath(W))
            add(side + "2", "dve", lambda: g.vector.tensor_tensor(buf(side + "2"), win.indirect(lst), buf(side + "1"), op),
                k2 + [key(side + "1")], [key(side + "2")], gath(W))
        pair("s", lambda: g.scalar.activation(buf("s1"), T.mt[:, :].indirect(fL), F.Copy), MT + [kF],
             T.sqt[:, :], eL, SQT + [kE], A.mult)
        pair("a", lambda: g.scalar.activation(buf("a1"), vt.indirect(eL), F.Abs, bias=0.25), ["vt", kE], vt, fL, ["vt", kF], A.add)
        add("a3", "act", lambda: g.scalar.activation(buf("a3"), buf("a2"), F.Abs, bias=-16.0), [key("a2")], [key("a3")], plain(W))

        def f_x():
            ins = None
            for a in range(8):
                ins = g.tensor.matmul(X, rowsum(0, a), buf("s2", a, 8), a == 0, a == 7)
            return ins
        add("mx", "pe", f_x, ["zm0", key("s2")], [kP], 8 * mm(N2))
        add("xh", "dve", lambda: g.vector.tensor_scalar(small("xh"), X, -1.0, None, A.mult), [], [kP, key("xh")], plain(N2))

        def f_prop():
            x0, x1 = small("xh", 0, 2), small("xh", 1, 2)
            g.tensor.matmul(P[:, 2 * N2:2 * N2 + NC], mat(LO, 0), x0, True, False)
            g.tensor.matmul(P[:, 2 * N2:2 * N2 + NC], mat(LO, 8), x1, False, True)
            g.tensor.matmul(P[:, 2 * N2 + NC:3 * N2], mat(HI, -8), x0, True, False)
            return g.tensor.matmul(P[:, 2 * N2 + NC:3 * N2], mat(HI, 0), x1, False, True)
        add("mprop", "pe", f_prop, ["pm0", "pm1", key("xh")], [kP], 4 * mm(NC))
        add("prop", "dve", lambda: g.vector.tensor_scalar(small("prop"), P[:, 2 * N2:3 * N2], 2048.0, None, A.add),
            [], [kP, key("prop")], plain(N2))
        if r:
            add("old", "dve", lambda: g.vector.tensor_scalar(small("old"), small("lst"), -1.0, 2048.0, A.mult, A.add), [kE], [kO],
                plain(N2, 0.5))

        def f_d():
            d0, d1 = P[:, 0:2 * N2:4], P[:, 2:2 * N2:4]
            oE, oF = O[:, e0:e0 + NC], O[:, f0:f0 + NC]
            g.tensor.matmul(P[:, 0:2 * N2:2], mat(ID, 0), small("xh"), True, False)
            g.tensor.matmul(d0, mat(LO, 0), oE, False, False)
            g.tensor.matmul(d0, mat(LO, 8), oF, False, False)
            g.tensor.matmul(d1, mat(HI, -8), oE, False, False)
            return g.tensor.matmul(d1, mat(HI, 0), oF, False, True)
        add("md", "pe", f_d, ["pm0", "pm1", "pm2", key("xh"), kO], [kP], 4 * mm(NC) + mm(N2))
        pair("b", lambda: g.scalar.activation(buf("b1"), vt.indirect(PR[:, l0:l0 + NC]), F.Abs, bias=0.25), ["vt", key("prop")],
             vt, PR[:, l0 + NC:l0 + N2], ["vt", key("prop")], A.add)
        add("b3r", "dve", lambda: g.vector.tensor_scalar(buf("b3"), buf("b2"), 16.0, -8.0, A.max, A.add), [key("b2")], [key("b3")],
            plain(W, 0.5))
        for nm, k in (("a3", 0), ("b2", 0), ("b3", 1)):
            def f_pack(nm=nm, k=k):
                g.tensor.matmul(B[:, 0:4 * N2], packer(k, 0), buf(nm, 0, 2), nm == "a3", False)
                return g.tensor.matmul(B[:, 0:4 * N2], packer(k, 1), buf(nm, 1, 2), False, nm == "b3")
            add("mp" + nm, "pe", f_pack, ["zd%d" % k, key(nm)], [kB], 2 * mm(4 * N2))
        add("ne", "act", lambda: g.scalar.activation(ne[:, h0:h0 + 4 * N2], B[:, 0:4 * N2], F.Abs), [], [kB, key("ne")], plain(4 * N2))

        def f_cnt():
            ins = None
            for b in range(4):
                ins = g.tensor.matmul(P[:, 3 * N2:4 * N2], rowsum(1, 2 * b), ne[:, h0 + b:h0 + 4 * N2:4], b == 0, b == 3)
            return ins
        add("mcnt", "pe", f_cnt, ["zm1", key("ne")], [kP], 4 * mm(N2))
        add("ok", "dve", lambda: g.vector.tensor_scalar(T.okb[:, 2 * l0 + 1:2 * (l0 + N2):2], P[:, 3 * N2:4 * N2], 0.0, None, A.is_gt),
            ["okb"], [kP, "ok%d" % c], plain(N2))
        new = T["new%d" % r]
        add("new", "dve", lambda: g.vector.tensor_tensor_scan(new[:, 2 * l0:2 * (l0 + N2)], T.okb[:, 2 * l0:2 * (l0 + N2)],
                                                              P[:, 0:2 * N2], 0.0, A.mult, A.add),
            ["ok%d" % c], [kP, key("new")], plain(2 * N2))
        n0 = 4 * N2

        def f_move():
            ins = None
            x = [new[:, 2 * (l0 + u) + 1:2 * (l0 + N2):4] for u in range(2)]
            rot = 16 * (c % 2)
            if r == RO - 1:
                way = [(P[:, n0 + h:n0 + N2:2],
                        [(LOP + h, 1 - h, 0), (LOP + h, 9 - h, 1), (HIP + h, -6 - h, 0), (FBP + h, -h, 1)]) for h in range(2)]
            elif r % 2 == 0:
                way = [(P[:, n0:n0 + NC], [(HI, -8, 0), (HI, 0, 1)]), (P[:, n0 + NC:n0 + N2], [(FA, 0, 0), (LO, 6, 1)])]
            else:
                way = [(P[:, n0:n0 + NC], [(HI, -6, 0), (FB, 0, 1)]), (P[:, n0 + NC:n0 + N2], [(LO, 0, 0), (LO, 8, 1)])]
            for o, parts in way:
                for j, (k, sh, u) in enumerate(parts):
                    ins = g.tensor.matmul(o, mat(k, sh + rot), x[u], j == 0, j == len(parts) - 1)
            return ins
        mats = range(LOP, FBP + 2) if r == RO - 1 else (LO, HI, FA if r % 2 == 0 else FB)
        add("mmove", "pe", f_move, ["pm%d" % k for k in mats] + [key("new")], [kP], (8 if r == RO - 1 else 4) * mm(NC))
        add("snd", "dve", lambda: g.vector.tensor_scalar(small("snd"), P[:, n0:n0 + N2], -1.0, 2048.0, A.mult, A.add), [],
            [kP, key("snd")], plain(N2))
        land = T["lst%d" % (r + 1)][:, l0:l0 + N2]
        i = add("rem", "pool",
                lambda: g.remote_dma(land, small("snd"), T.sem["arr%d_%d" % (r, c)], T.sem.sent, dst_addr[1], dst_addr[0], out_mask),
                [key("snd")], [], cost["issue"], 0.0, ("remote", 0))
        add("arr", "none", None, [], ["l%d_%d" % (r + 1, c)], 0.0, cost["remote"] + (cost["first"] if seq[0] == 0 else 0.0),
            ("arr%d_%d" % (r, c), n_in), after=[i])

    def last_chunk(c):
        c0 = C0[c]
        l0, y0, y1 = 2 * c0, 2 * (c0 % 64), 2 * (c0 % 64 + NC)
        w0, w1 = 32 * c0, 32 * (c0 + NC)
        L, kL = T["lst%d" % RO][:, l0:l0 + N2], "l%d_%d" % (RO, c)
        for h in range(2):
            add("zyc", "dve", lambda h=h: g.vector.tensor_copy(T.ycs[:, 2 * y0 + 2 * (c % 2) + h:2 * y1:4],
                                                               T["lst%d" % RO][:, l0 + h:l0 + N2:2]),
                [kL], ["yc%d_%d" % (c, h)], plain(NC))
        if c % 2:
            add("zoc", "sync", lambda: g.sync.dma_start(T.yc[:, 2 * y0:2 * y1], T.ycs[:, 2 * y0:2 * y1]),
                ["yc%d_%d" % (k, h) for k in (c - 1, c) for h in range(2)], [], 400.0, cost["dma"], ("outs", 0))
        sg, dd, fx = "sg%d" % c, "dd%d" % c, T.fx[:, c0:c0 + NC]
        add("zs", "act", lambda: g.scalar.activation(T.sg[:, w0:w1], vt.indirect(L), F.Sign), ["vt", kL], [sg], gath(32 * NC))
        add("zx", "dve", lambda: g.vector.tensor_scalar(T.dd[:, w0:w1], vt.indirect(L), -16.0, None, A.add), ["vt", kL], [dd],
            gath(32 * NC))
        add("zf", "act", lambda: g.scalar.activation(fx, T.sg[:, w0 + 31:w1:32], F.Identity, scale=-16.0), [sg], ["fx%d" % c], plain(NC))
        add("zf", "dve", lambda: g.vector.memset(T.sg[:, w0 + 31:w1:32], 0.0), [], [sg], plain(NC))
        add("zf", "dve", lambda: g.vector.tensor_tensor(T.dd[:, w0 + 31:w1:32], T.dd[:, w0 + 31:w1:32], fx, A.add),
            ["fx%d" % c], [dd], plain(NC, 2.0))

        def rev(b):
            return b[:, w1 - 1::-1] if w0 == 0 else b[:, w1 - 1:w0 - 1:-1]
        add("zscan", "dve", lambda: g.vector.tensor_tensor_scan(rev(T.hs), rev(T.sg), rev(T.dd), 0.0, A.mult, A.add),
            [sg, dd], ["hs%d" % c], plain(32 * NC, 0.5))
        add("zyb", "act", lambda: g.scalar.activation(T.ybs[:, y0 + c % 2:y1:2], T.hs[:, w0:w1:32], F.Identity, bias=16.0),
            ["hs%d" % c], ["yb%d" % c], plain(NC))
        if c % 2:
            add("zob", "sync", lambda: g.sync.dma_start(T.yb[:, y0:y1], T.ybs[:, y0:y1]), ["yb%d" % (c - 1), "yb%d" % c], [],
                400.0, cost["dma"], ("outs", 0))

    for r in range(RO):
        for c in range(NCH):
            seq[0] = r * NCH + c
            round_chunk(r, c)
    for c in range(NCH):
        seq[0] = RO * NCH + c
        last_chunk(c)
    return ops


def run_through(order, eng, deps, dur, lat):
    free, last = [0.0] * 6, [-1] * 6
    end, pred, queued = [0.0] * len(dur), [-1] * len(dur), [False] * len(dur)
    for i in order:
        e = eng[i]
        t, p, q = free[e], last[e], True
        for d, hop in deps[i]:
            if end[d] + hop > t:
                t, p, q = end[d] + hop, d, False
        pred[i], queued[i] = p, q
        if e != 5:
            free[e], last[e] = t + dur[i], i
        end[i] = t + dur[i] + lat[i]
    total = max(end)
    i, pairs = end.index(total), []
    while pred[i] >= 0:
        if queued[i]:
            pairs.append((pred[i], i))
        i = pred[i]
    return total, pairs


def plan(steps, costs):
    ops = steps[0]
    n = len(ops)
    rank = []
    for i, o in enumerate(ops):
        own = max(o["seq"], 0) + STAGE[o["typ"]] + SHIFT.get((o["typ"], o["seq"]), 0.0) + 1e-5 * i
        rank.append(max([own] + [rank[d] + 1e-5 for d in o["deps"]]))
    order = sorted(range(n), key=lambda i: rank[i])
    eng = [["act", "dve", "pe", "pool", "sync", "none"].index(o["eng"]) for o in ops]
    users = [set() for _ in ops]
    for i, o in enumerate(ops):
        for d in o["deps"]:
            users[d].add(i)

    def wait(i, d, c):
        if eng[i] == 5 or eng[i] == eng[d] == 2:
            return 0.0
        return c["wake"] if eng[d] == 5 or d < LOADS else c["same"] if eng[i] == eng[d] else c["pehop"] if eng[d] == 2 else c["hop"]
    data = [([[(d, wait(i, d, c)) for d in o["deps"]] for i, o in enumerate(s)],
             [o["dur"] for o in s], [o["lat"] for o in s]) for s, c in zip(steps, costs)]
    seed = [SEED]

    def draw():
        seed[0] = (seed[0] * 6364136223846793005 + 1442695040888963407) % 2 ** 64
        return (seed[0] >> 11) / 2.0 ** 53

    def score(o):
        runs = [run_through(o, eng, *d) for d in data]
        return sum(math.log(r[0]) for r in runs) / len(runs), runs
    now, runs = score(order)
    best = (now, order)
    for turn in range(TURNS):
        pairs = runs[int(draw() * len(runs))][1]
        if not pairs:
            continue
        u, v = pairs[int(draw() * len(pairs))]
        a = order.index(u)
        if draw() < 0.3:
            a = max([k for k in range(a) if eng[order[k]] == eng[u]] or [a])
        b = order.index(v)
        need = {v}
        for x in order[b - 1:a - 1 if a else None:-1]:
            if users[x] & need:
                need.add(x)
        if order[a] in need:
            continue
        part = order[a:b + 1]
        trial = order[:a] + [x for x in part if x in need] + [x for x in part if x not in need] + order[b + 1:]
        loads = [x for x in trial[:b + 1] if x < LOADS]
        if loads != list(range(len(loads))):
            continue
        s, r = score(trial)
        if s <= now or draw() < math.exp((now - s) / (HEAT * (1 - turn / TURNS) + 1e-6)):
            order, now, runs = trial, s, r
            if s < best[0]:
                best = (s, order)
    return best[1]


def waits(ops, order):
    count = {"act": 0, "dve": 0, "pe": 0, "pool": 0}
    place = {i: k for k, i in enumerate(order)}
    done, knew, seen, need = {}, {}, {}, {}
    for i in order:
        o = ops[i]
        e = o["eng"]
        need[i] = []
        if e == "none":
            done[i], knew[i] = o["sem"], {}
            continue
        known = seen.setdefault(e, {})
        for d in sorted(o["deps"], key=lambda d: -place[d]):
            s, val = done[d]
            if not (e == "pe" and ops[d]["eng"] == "pe") and known.get(s, 0) < val:
                need[i].append((s, val))
                known[s] = val
                for k, w in knew[d].items():
                    known[k] = max(known.get(k, 0), w)
        knew[i] = dict(known)
        if o["sem"] is None:
            count[e] += 1
            done[i] = ("c_" + e, count[e])
        else:
            done[i] = o["sem"]
    return need, count


PLAN = []


def rank_program(g, core, T, topo):
    rank = T.rank_of(core)
    if rank is None:
        return
    n = len(T.cores)
    dst = T.cores[(rank + 3) % n]
    src = T.cores[(rank - 3) % n]
    out_mask = topo.mask(core, dst)
    n_out = len(topo.engines(core, dst))
    n_in = len(topo.engines(src, core))
    steps = [build(T, g, topo.addr(dst, core), out_mask, n_in, c) for c in COSTS]
    if not PLAN:
        PLAN.extend(plan(steps, COSTS))
    ops = steps[0]
    need, count = waits(ops, PLAN)
    queue = {"act": g.scalar, "dve": g.vector, "pe": g.tensor, "pool": g, "sync": g.sync}
    outs = 0
    sent = 0
    for i in PLAN:
        o = ops[i]
        e = o["eng"]
        if e == "none":
            continue
        for s, val in need[i]:
            queue[e].wait_ge(T.sem[s], val)
        ins = o["fn"]()
        if o["sem"] is None:
            ins.then_inc(T.sem["c_" + e], 1)
        elif o["sem"][0] == "remote":
            sent += n_out
        else:
            ins.then_inc(T.sem[o["sem"][0]], 16)
            if o["sem"][0] == "outs":
                outs += 16
    for e in ("pool", "pe", "dve", "act"):
        g.wait_ge(T.sem["c_" + e], count[e])
    g.wait_ge(T.sem.sent, sent)
    g.sync.wait_ge(T.sem.outs, outs)
